import numpy as np
import ml_dtypes


def mxq(x, axis, fmt="e4m3"):
    dtype, down = {"e4m3": (ml_dtypes.float8_e4m3fn, 7), "e5m2": (ml_dtypes.float8_e5m2, 14)}[fmt]
    v = np.moveaxis(np.asarray(x, np.float32).astype(ml_dtypes.bfloat16).astype(np.float64), axis, -1)
    blocks = v.reshape(v.shape[:-1] + (-1, 32))
    amax = np.abs(blocks).max(-1, keepdims=True)
    byte = np.maximum(np.where(amax > 0, np.frexp(amax)[1] - 1 + 127, 0) - down, 1)
    scale = np.exp2(byte - 127.0)
    codes = (blocks / scale).astype(np.float32).astype(dtype).astype(np.float64)
    return np.moveaxis((codes * scale).reshape(v.shape), -1, axis)


WIDE = False


def mx_kscale(k):
    if not WIDE:
        return np.ones(k)
    levels = np.array([10, -10, 5, -5, 0])
    if k % 512:
        return np.exp2(np.random.permutation(np.resize(levels, k // 32))).repeat(32)
    a = np.empty((k // 512, 16))
    for p in range(k // 512):
        a[p, :8] = np.random.permutation(np.resize(levels, 8))
        for g in range(8):
            far = levels[np.abs(levels - a[p, g]) >= 10]
            a[p, g + 8] = far[np.random.randint(len(far))]
    return np.exp2(a.ravel()).repeat(32)


def f64(x):
    return np.asarray(x).astype(np.float64)


def striped8(idx):
    return np.concatenate([x.reshape(-1, 16).T for x in idx]).astype(np.uint16)


def runs(offs, k):
    lists = np.stack([offs[16 * r : 16 * r + 16].T.reshape(-1) for r in range(8)]).astype(np.int64)
    return lists[np.arange(k) % 512 // 64]


def pack_weight(w):
    k, n = w.shape
    w = f64(np.asarray(w, np.float32).astype(ml_dtypes.bfloat16)).reshape(k // 32, 32, n)
    amax = np.abs(w).max(1)
    byte = np.clip(np.where(amax > 0, np.frexp(amax)[1] - 1 + 127 - 7, 1), 1, 254)
    scaled = (w * np.exp2(127.0 - byte)[:, None, :]).reshape(k, n).astype(np.float32)
    words = np.ascontiguousarray(scaled.reshape(k // 512, 128, 4, n).transpose(0, 1, 3, 2)).astype(ml_dtypes.float8_e4m3fn).view(np.uint8)
    return words, np.ascontiguousarray(byte.astype(np.uint8).reshape(k // 512, 16, n))


def unpack_weight(words, scales):
    g, p, n, _ = words.shape
    vals = np.ascontiguousarray(words).view(ml_dtypes.float8_e4m3fn).astype(np.float64) * np.repeat(np.exp2(scales.astype(np.float64) - 127.0), 8, axis=1)[..., None]
    return vals.transpose(0, 1, 3, 2).reshape(g * 512, n)


def silu(v):
    return v / (1.0 + np.exp(-np.maximum(v, -700.0)))

def planes(y):
    n, m = y.shape
    v = y.astype(np.float32).astype(ml_dtypes.bfloat16).astype(np.float64).reshape(n // 32, 32, m)
    top = np.abs(v).max(1)
    byte = np.clip(np.where(top > 0, np.frexp(top)[1] - 1 + 127 - 7, 1), 1, 254)
    codes = (v * np.exp2(127.0 - byte)[:, None, :]).reshape(n, m).astype(np.float32).astype(ml_dtypes.float8_e4m3fn).view(np.uint8)
    words = codes.reshape(n // 512, 128, 4, m).transpose(0, 1, 3, 2)
    return np.ascontiguousarray(words), np.ascontiguousarray(byte.astype(np.uint8).reshape(n // 512, 16, m))


K, T, S, N = 512, 2048, 512, 512


def setup_inputs():
    n = np.random.standard_normal
    s = mx_kscale(K)[:, None]
    packed_xT = pack_weight(n((K, T)) * s)
    return {
        "x_words": packed_xT[0],
        "x_scales": packed_xT[1],
        "w1": (n((K, N)) / np.sqrt(K) / s).astype(np.float32),
        "w2": (n((K, N)) / np.sqrt(K) / s).astype(np.float32),
        "offs": striped8(np.stack([np.random.permutation(T)[:S] for _ in range(8)])),
    }


def reference(x_words, x_scales, w1, w2, offs):
    xq = unpack_weight(x_words, x_scales)[np.arange(K)[:, None], runs(offs, K)]
    out_0 = (silu(mxq(f64(w1), 0, "e4m3").T @ xq)) * ((mxq(f64(w2), 0, "e4m3").T @ xq))
    return (out_0,) + planes(out_0)

@@ -1,0 +1,151 @@
+from contextlib import ExitStack
+
+import concourse.mybir as mybir
+
+K, T, S, N = 512, 2048, 512, 512
+FLOPS = 2 * 2 * K * N * S
+
+F32 = mybir.dt.float32
+BF16 = mybir.dt.bfloat16
+I32 = mybir.dt.int32
+U32 = mybir.dt.uint32
+U16 = mybir.dt.uint16
+U8 = mybir.dt.uint8
+FP8X4 = mybir.dt.float8_e4m3fn_x4
+SILU = mybir.ActivationFunctionType.Silu
+MULT = mybir.AluOpType.mult
+
+P = 128
+PACK = 4
+QUARTER = 128
+HALF = 256
+M_VECTOR = 84
+
+
+def tile_picked_phglu_silu_po_kernel(
+    tc, x_words, x_scales, w1, w2, offs, out_0, out_1, out_2
+):
+    nc = tc.nc
+    with ExitStack() as ctx:
+        keep = ctx.enter_context(tc.tile_pool(name="keep", bufs=1))
+        psum = ctx.enter_context(tc.psum_pool(name="psum", bufs=1))
+
+        offsets = keep.tile([P, S // 16], U16, name="offsets")
+        nc.sync.dma_start(offsets[:], offs)
+
+        scale_table = keep.tile([P, T], U8, name="scale_table", align_bytes=64)
+        nc.vector.memset(scale_table[:].bitcast(I32), 0)
+        nc.scalar.dma_start(out=scale_table[0:P:8, :].bitcast(I32), in_=x_scales[0].bitcast(I32))
+
+        warm_in = keep.tile([P, 1], F32, name="warm_in")
+        warm_out = keep.tile([P, 1], F32, name="warm_out")
+        nc.gpsimd.memset(warm_in[:], 0.0)
+        nc.scalar.activation(out=warm_out[:], in_=warm_in[:], func=SILU)
+
+        word_table = keep.tile([P, T], U32, name="word_table", align_bytes=64)
+        raw = [keep.tile([P, PACK, N], F32, name="raw%d" % i, align_bytes=64) for i in range(2)]
+
+        def load_w(i, w):
+            nc.sync.dma_start(out=raw[i][:], in_=w.rearrange("(p j) c -> p j c", j=PACK))
+
+        def load_x():
+            nc.sync.dma_start(
+                out=word_table[:].bitcast(I32), in_=x_words[0].rearrange("p c r -> p (c r)").bitcast(I32)
+            )
+
+        load_w(0, w1)
+        load_x()
+        load_w(1, w2)
+
+        picked_scales = keep.tile([P, S], U8, name="picked_scales", align_bytes=64)
+        nc.vector.tensor_copy(out=picked_scales[:], in_=scale_table[:].indirect(offsets[:]))
+        x_plane = keep.tile([P, S], U8, name="x_plane", align_bytes=64)
+        nc.vector.tensor_copy(out=x_plane[:].bitcast(I32), in_=picked_scales[:].bitcast(I32))
+        for s in range(1, 4):
+            nc.scalar.dma_start(
+                out=x_plane[s:P:32, :].bitcast(I32), in_=picked_scales[8 * s : P : 32, :].bitcast(I32)
+            )
+
+        def quantize_w(i):
+            grouped = keep.tile([P, PACK, P, PACK], BF16, name="grouped%d" % i, align_bytes=64)
+            dst = grouped[:].rearrange("p t m j -> p m t j")
+            src = raw[i][:].rearrange("p j (m t) -> p m t j", t=PACK)
+            nc.vector.tensor_copy(out=dst[:, :M_VECTOR], in_=src[:, :M_VECTOR])
+            nc.scalar.copy(out=dst[:, M_VECTOR:], in_=src[:, M_VECTOR:])
+            codes = keep.tile([P, N], U32, name="w_codes%d" % i, align_bytes=64)
+            plane = keep.tile([P, N], U8, name="w_plane%d" % i, align_bytes=64)
+            flat = grouped[:].rearrange("p t m j -> p (t m j)")
+            for t in range(0, PACK, 2):
+                nc.vector.quantize_mx(
+                    out=codes[:, t * P : (t + 2) * P].bitcast(FP8X4),
+                    scales=plane[:, t * P : (t + 2) * P],
+                    in_=flat[:, t * N : (t + 2) * N],
+                )
+            return codes, plane
+
+        def gather_x():
+            halves = []
+            for h in range(2):
+                picked = keep.tile([P, HALF], U32, name="picked%d" % h, align_bytes=64)
+                nc.vector.tensor_copy(
+                    out=picked[:], in_=word_table[:].indirect(offsets[:, h * HALF // 16 : (h + 1) * HALF // 16])
+                )
+                halves.append(picked)
+            return halves
+
+        def product(i, q, codes, plane, halves):
+            bank = psum.tile([P, PACK, QUARTER], F32, name="bank%d_%d" % (i, q))
+            lo = (q % 2) * QUARTER
+            for t in range(PACK):
+                nc.tensor.matmul_mx(
+                    out=bank[:, t, :],
+                    lhsT=codes[:, t * P : (t + 1) * P].bitcast(FP8X4),
+                    lhsT_scale=plane[:, t * P : (t + 1) * P],
+                    rhs=halves[q // 2][:, lo : lo + QUARTER].bitcast(FP8X4),
+                    rhs_scale=x_plane[:, q * QUARTER : (q + 1) * QUARTER],
+                    start=True,
+                    stop=True,
+                )
+            return bank
+
+        codes1, plane1 = quantize_w(0)
+        halves = gather_x()
+        gates = []
+        for q in range(4):
+            bank = product(0, q, codes1, plane1, halves)
+            gate = keep.tile([P, PACK, QUARTER], F32, name="gate%d" % q, align_bytes=64)
+            nc.scalar.activation(out=gate[:], in_=bank[:], func=SILU)
+            gates.append(gate)
+        codes2, plane2 = quantize_w(1)
+
+        y_rows = out_0.rearrange("(p t) j -> p t j", t=PACK)
+        y_words = out_1[0].rearrange("p c r -> p (c r)").bitcast(I32)
+        y_plane = keep.tile([P, S], U8, name="y_plane", align_bytes=64)
+        for h in range(2):
+            y = keep.tile([P, PACK, HALF], F32, name="y%d" % h, align_bytes=64)
+            y_codes = keep.tile([P, HALF], U32, name="y_codes%d" % h, align_bytes=64)
+            for u in range(2):
+                q = 2 * h + u
+                cols = slice(u * QUARTER, (u + 1) * QUARTER)
+                bank = product(1, q, codes2, plane2, halves)
+                nc.vector.tensor_tensor(out=y[:, :, cols], in0=bank[:], in1=gates[q][:], op=MULT)
+                rounded = keep.tile([P, QUARTER, PACK], BF16, name="rounded%d" % q, align_bytes=64)
+                dst = rounded[:].rearrange("p (c i) t -> p c t i", i=4)
+                src = y[:, :, cols].rearrange("p t (c i) -> p c t i", i=4)
+                if q == 3:
+                    nc.vector.tensor_copy(out=dst, in_=src)
+                else:
+                    nc.scalar.copy(out=dst, in_=src)
+                nc.vector.quantize_mx(
+                    out=y_codes[:, cols].bitcast(FP8X4),
+                    scales=y_plane[:, q * QUARTER : (q + 1) * QUARTER],
+                    in_=rounded[:].rearrange("p c t -> p (c t)"),
+                )
+            nc.sync.dma_start(out=y_rows[:, :, h * HALF : (h + 1) * HALF], in_=y[:])
+            nc.sync.dma_start(out=y_words[:, h * HALF : (h + 1) * HALF], in_=y_codes[:].bitcast(I32))
+        for quad in range(4):
+            queue = nc.sync if quad % 2 == 0 else nc.scalar
+            queue.dma_start(
+                out=out_2[0, 4 * quad : 4 * quad + 4, :].bitcast(I32),
+                in_=y_plane[32 * quad : 32 * quad + 4, :].bitcast(I32),
+            )

@@ -19,7 +19,6 @@ P = 128
 PACK = 4
 QUARTER = 128
 HALF = 256
-M_VECTOR = 84
 
 
 def tile_picked_phglu_silu_po_kernel(
@@ -30,108 +29,124 @@ def tile_picked_phglu_silu_po_kernel(
         keep = ctx.enter_context(tc.tile_pool(name="keep", bufs=1))
         psum = ctx.enter_context(tc.psum_pool(name="psum", bufs=1))
 
+        raw1 = keep.tile([P, PACK, N], F32, name="raw1", align_bytes=64)
+        w1_rows = w1.rearrange("(p j) c -> p j c", j=PACK)
+        nc.sync.dma_start(out=raw1[:, 0:1, :], in_=w1_rows[:, 0:1, :])
         offsets = keep.tile([P, S // 16], U16, name="offsets")
         nc.sync.dma_start(offsets[:], offs)
 
-        scale_table = keep.tile([P, T], U8, name="scale_table", align_bytes=64)
+        scale_table = keep.tile([P, T], U8, name="scale_table", tag="shared", align_bytes=64)
         nc.vector.memset(scale_table[:].bitcast(I32), 0)
-        nc.scalar.dma_start(out=scale_table[0:P:8, :].bitcast(I32), in_=x_scales[0].bitcast(I32))
+        nc.sync.dma_start(out=scale_table[0:P:8, :].bitcast(I32), in_=x_scales[0].bitcast(I32))
 
-        warm_in = keep.tile([P, 1], F32, name="warm_in")
-        warm_out = keep.tile([P, 1], F32, name="warm_out")
-        nc.gpsimd.memset(warm_in[:], 0.0)
-        nc.scalar.activation(out=warm_out[:], in_=warm_in[:], func=SILU)
 
+        nc.sync.dma_start(out=raw1[:, 1:4, :], in_=w1_rows[:, 1:4, :])
         word_table = keep.tile([P, T], U32, name="word_table", align_bytes=64)
-        raw = [keep.tile([P, PACK, N], F32, name="raw%d" % i, align_bytes=64) for i in range(2)]
-
-        def load_w(i, w):
-            nc.sync.dma_start(out=raw[i][:], in_=w.rearrange("(p j) c -> p j c", j=PACK))
-
-        def load_x():
-            nc.sync.dma_start(
-                out=word_table[:].bitcast(I32), in_=x_words[0].rearrange("p c r -> p (c r)").bitcast(I32)
-            )
-
-        load_w(0, w1)
-        load_x()
-        load_w(1, w2)
+        nc.sync.dma_start(
+            out=word_table[:].bitcast(I32), in_=x_words[0].rearrange("p c r -> p (c r)").bitcast(I32)
+        )
 
         picked_scales = keep.tile([P, S], U8, name="picked_scales", align_bytes=64)
         nc.vector.tensor_copy(out=picked_scales[:], in_=scale_table[:].indirect(offsets[:]))
         x_plane = keep.tile([P, S], U8, name="x_plane", align_bytes=64)
-        nc.vector.tensor_copy(out=x_plane[:].bitcast(I32), in_=picked_scales[:].bitcast(I32))
-        for s in range(1, 4):
-            nc.scalar.dma_start(
-                out=x_plane[s:P:32, :].bitcast(I32), in_=picked_scales[8 * s : P : 32, :].bitcast(I32)
+        nc.gpsimd.memset(x_plane[:].bitcast(I32), 0)
+        for quad in range(4):
+            nc.sync.dma_start(
+                out=x_plane[32 * quad : 32 * quad + 4, :].bitcast(I32),
+                in_=picked_scales[32 * quad : 32 * quad + 32 : 8, :].bitcast(I32),
             )
+        raw2 = keep.tile([P, PACK, N], F32, name="raw2", tag="shared", align_bytes=64)
+        w2_rows = w2.rearrange("(p j) c -> p j c", j=PACK)
+        for j in (0, 2):
+            nc.sync.dma_start(out=raw2[:, j : j + 2, :], in_=w2_rows[:, j : j + 2, :])
 
-        def quantize_w(i):
-            grouped = keep.tile([P, PACK, P, PACK], BF16, name="grouped%d" % i, align_bytes=64)
-            dst = grouped[:].rearrange("p t m j -> p m t j")
-            src = raw[i][:].rearrange("p j (m t) -> p m t j", t=PACK)
-            nc.vector.tensor_copy(out=dst[:, :M_VECTOR], in_=src[:, :M_VECTOR])
-            nc.scalar.copy(out=dst[:, M_VECTOR:], in_=src[:, M_VECTOR:])
-            codes = keep.tile([P, N], U32, name="w_codes%d" % i, align_bytes=64)
-            plane = keep.tile([P, N], U8, name="w_plane%d" % i, align_bytes=64)
-            flat = grouped[:].rearrange("p t m j -> p (t m j)")
-            for t in range(0, PACK, 2):
+        def quantize_w(grouped, name):
+            codes = keep.tile([P, N], U32, name="w_codes" + name, align_bytes=64)
+            plane = keep.tile([P, N], U8, name="w_plane" + name, align_bytes=64)
+            for t in range(PACK):
+                cols = slice(t * P, (t + 1) * P)
                 nc.vector.quantize_mx(
-                    out=codes[:, t * P : (t + 2) * P].bitcast(FP8X4),
-                    scales=plane[:, t * P : (t + 2) * P],
-                    in_=flat[:, t * N : (t + 2) * N],
+                    out=codes[:, cols].bitcast(FP8X4),
+                    scales=plane[:, cols],
+                    in_=grouped[t].rearrange("p m j -> p (m j)"),
                 )
             return codes, plane
 
-        def gather_x():
-            halves = []
-            for h in range(2):
-                picked = keep.tile([P, HALF], U32, name="picked%d" % h, align_bytes=64)
-                nc.vector.tensor_copy(
-                    out=picked[:], in_=word_table[:].indirect(offsets[:, h * HALF // 16 : (h + 1) * HALF // 16])
-                )
-                halves.append(picked)
-            return halves
+        grouped1 = keep.tile([P, PACK, P, PACK], BF16, name="grouped1", tag="grouped1", align_bytes=64)
+        nc.vector.tensor_copy(
+            out=grouped1[:].rearrange("p t m j -> p m t j"), in_=raw1[:].rearrange("p j (m t) -> p m t j", t=PACK)
+        )
+        codes1, plane1 = quantize_w([grouped1[:, t] for t in range(PACK)], "1")
 
-        def product(i, q, codes, plane, halves):
-            bank = psum.tile([P, PACK, QUARTER], F32, name="bank%d_%d" % (i, q))
-            lo = (q % 2) * QUARTER
-            for t in range(PACK):
-                nc.tensor.matmul_mx(
-                    out=bank[:, t, :],
-                    lhsT=codes[:, t * P : (t + 1) * P].bitcast(FP8X4),
-                    lhsT_scale=plane[:, t * P : (t + 1) * P],
-                    rhs=halves[q // 2][:, lo : lo + QUARTER].bitcast(FP8X4),
-                    rhs_scale=x_plane[:, q * QUARTER : (q + 1) * QUARTER],
-                    start=True,
-                    stop=True,
-                )
+        picked = keep.tile([P, S], U32, name="picked", tag="grouped1", align_bytes=64)
+        for h in range(2):
+            nc.vector.tensor_copy(
+                out=picked[:, h * HALF : (h + 1) * HALF],
+                in_=word_table[:].indirect(offsets[:, h * HALF // 16 : (h + 1) * HALF // 16]),
+            )
+
+        blocks = ((0, 1, 0, S), (1, 1, 0, S), (2, 2, 0, HALF), (2, 2, HALF, HALF))
+
+        def product(name, block, codes, plane, width):
+            t0, nt, c0, nc_cols = block
+            bank = psum.tile([P, nt, nc_cols], F32, name="bank%s_%d_%d" % (name, t0, c0))
+            for t in range(t0, t0 + nt):
+                for lo in range(0, nc_cols, width):
+                    n = min(width, nc_cols)
+                    nc.tensor.matmul_mx(
+                        out=bank[:, t - t0, lo : lo + n],
+                        lhsT=codes[:, t * P : (t + 1) * P].bitcast(FP8X4),
+                        lhsT_scale=plane[:, t * P : (t + 1) * P],
+                        rhs=picked[:, c0 + lo : c0 + lo + n].bitcast(FP8X4),
+                        rhs_scale=x_plane[:, c0 + lo : c0 + lo + n],
+                        start=True,
+                        stop=True,
+                    )
             return bank
 
-        codes1, plane1 = quantize_w(0)
-        halves = gather_x()
         gates = []
-        for q in range(4):
-            bank = product(0, q, codes1, plane1, halves)
-            gate = keep.tile([P, PACK, QUARTER], F32, name="gate%d" % q, align_bytes=64)
+        for b, block in enumerate(blocks):
+            bank = product("1", block, codes1, plane1, HALF)
+            gate = keep.tile([P, block[1], block[3]], F32, name="gate%d" % b, align_bytes=64)
             nc.scalar.activation(out=gate[:], in_=bank[:], func=SILU)
             gates.append(gate)
-        codes2, plane2 = quantize_w(1)
+
+        pairs = [keep.tile([P, 2, P, PACK], BF16, name="pair%d" % u, align_bytes=64) for u in range(2)]
+        for j in (0, 2):
+            src = raw2[:, j : j + 2, :].rearrange("p j (m e t) -> p m t e j", e=2, t=PACK)
+            for u in range(2):
+                nc.vector.tensor_copy(
+                    out=pairs[u][:, :, :, j : j + 2].rearrange("p t (m e) j -> p m t e j", e=2),
+                    in_=src[:, :, 2 * u : 2 * u + 2],
+                )
+        codes2, plane2 = quantize_w([pairs[t // 2][:, t % 2] for t in range(PACK)], "2")
 
         y_rows = out_0.rearrange("(p t) j -> p t j", t=PACK)
         y_words = out_1[0].rearrange("p c r -> p (c r)").bitcast(I32)
         y_plane = keep.tile([P, S], U8, name="y_plane", align_bytes=64)
+        y = keep.tile([P, PACK, S], F32, name="y", align_bytes=64)
+        for b, block in enumerate(blocks):
+            t0, nt, c0, width = block
+            bank = product("2", block, codes2, plane2, S)
+            step = width // nt
+            for lo in range(0, width, step):
+                nc.vector.tensor_tensor(
+                    out=y[:, t0 : t0 + nt, c0 + lo : c0 + lo + step],
+                    in0=bank[:, :, lo : lo + step],
+                    in1=gates[b][:, :, lo : lo + step],
+                    op=MULT,
+                )
+            nc.sync.dma_start(
+                out=y_rows[:, t0 : t0 + nt, c0 : c0 + width], in_=y[:, t0 : t0 + nt, c0 : c0 + width]
+            )
         for h in range(2):
-            y = keep.tile([P, PACK, HALF], F32, name="y%d" % h, align_bytes=64)
             y_codes = keep.tile([P, HALF], U32, name="y_codes%d" % h, align_bytes=64)
             for u in range(2):
                 q = 2 * h + u
                 cols = slice(u * QUARTER, (u + 1) * QUARTER)
-                bank = product(1, q, codes2, plane2, halves)
-                nc.vector.tensor_tensor(out=y[:, :, cols], in0=bank[:], in1=gates[q][:], op=MULT)
                 rounded = keep.tile([P, QUARTER, PACK], BF16, name="rounded%d" % q, align_bytes=64)
                 dst = rounded[:].rearrange("p (c i) t -> p c t i", i=4)
-                src = y[:, :, cols].rearrange("p t (c i) -> p c t i", i=4)
+                src = y[:, :, q * QUARTER : (q + 1) * QUARTER].rearrange("p t (c i) -> p c t i", i=4)
                 if q == 3:
                     nc.vector.tensor_copy(out=dst, in_=src)
                 else:
@@ -141,7 +156,6 @@ def tile_picked_phglu_silu_po_kernel(
                     scales=y_plane[:, q * QUARTER : (q + 1) * QUARTER],
                     in_=rounded[:].rearrange("p c t -> p (c t)"),
                 )
-            nc.sync.dma_start(out=y_rows[:, :, h * HALF : (h + 1) * HALF], in_=y[:])
             nc.sync.dma_start(out=y_words[:, h * HALF : (h + 1) * HALF], in_=y_codes[:].bitcast(I32))
         for quad in range(4):
             queue = nc.sync if quad % 2 == 0 else nc.scalar

@@ -19,6 +19,7 @@ P = 128
 PACK = 4
 QUARTER = 128
 HALF = 256
+PAIR_BYTES = 2 * N * 4
 
 
 def tile_picked_phglu_silu_po_kernel(
@@ -27,7 +28,12 @@ def tile_picked_phglu_silu_po_kernel(
     nc = tc.nc
     with ExitStack() as ctx:
         keep = ctx.enter_context(tc.tile_pool(name="keep", bufs=1))
+        reuse = ctx.enter_context(tc.tile_pool(name="reuse", bufs=1))
         psum = ctx.enter_context(tc.psum_pool(name="psum", bufs=1))
+
+        warm = keep.tile([P, 2], F32, name="warm")
+        nc.gpsimd.memset(warm[:, 0:1], 0.0)
+        nc.scalar.activation(out=warm[:, 1:2], in_=warm[:, 0:1], func=SILU)
 
         raw1 = keep.tile([P, PACK, N], F32, name="raw1", align_bytes=64)
         w1_rows = w1.rearrange("(p j) c -> p j c", j=PACK)
@@ -35,7 +41,7 @@ def tile_picked_phglu_silu_po_kernel(
         offsets = keep.tile([P, S // 16], U16, name="offsets")
         nc.sync.dma_start(offsets[:], offs)
 
-        scale_table = keep.tile([P, T], U8, name="scale_table", tag="shared", align_bytes=64)
+        scale_table = reuse.tile([P, T], U8, name="scale_table", offset=2 * PAIR_BYTES - T // 2, align_bytes=64)
         nc.vector.memset(scale_table[:].bitcast(I32), 0)
         nc.sync.dma_start(out=scale_table[0:P:8, :].bitcast(I32), in_=x_scales[0].bitcast(I32))
 
@@ -55,10 +61,11 @@ def tile_picked_phglu_silu_po_kernel(
                 out=x_plane[32 * quad : 32 * quad + 4, :].bitcast(I32),
                 in_=picked_scales[32 * quad : 32 * quad + 32 : 8, :].bitcast(I32),
             )
-        raw2 = keep.tile([P, PACK, N], F32, name="raw2", tag="shared", align_bytes=64)
         w2_rows = w2.rearrange("(p j) c -> p j c", j=PACK)
+        raw2 = {}
         for j in (0, 2):
-            nc.sync.dma_start(out=raw2[:, j : j + 2, :], in_=w2_rows[:, j : j + 2, :])
+            raw2[j] = reuse.tile([P, 2, N], F32, name="raw2_%d" % j, offset=PAIR_BYTES * (1 + j // 2), align_bytes=64)
+            nc.sync.dma_start(out=raw2[j][:], in_=w2_rows[:, j : j + 2, :])
 
         def quantize_w(grouped, name):
             codes = keep.tile([P, N], U32, name="w_codes" + name, align_bytes=64)
@@ -72,11 +79,15 @@ def tile_picked_phglu_silu_po_kernel(
                 )
             return codes, plane
 
-        grouped1 = keep.tile([P, PACK, P, PACK], BF16, name="grouped1", tag="grouped1", align_bytes=64)
-        nc.vector.tensor_copy(
-            out=grouped1[:].rearrange("p t m j -> p m t j"), in_=raw1[:].rearrange("p j (m t) -> p m t j", t=PACK)
-        )
-        codes1, plane1 = quantize_w([grouped1[:, t] for t in range(PACK)], "1")
+        w1_pairs = [
+            keep.tile([P, 2, P, PACK], BF16, name="w1_pair", tag=tag, align_bytes=64) for tag in ("w1_pair", "grouped1")
+        ]
+        for u, copy in enumerate((nc.vector.tensor_copy, nc.scalar.copy)):
+            copy(
+                out=w1_pairs[u][:].rearrange("p t m j -> p m j t"),
+                in_=raw1[:].rearrange("p j (m t) -> p m j t", t=PACK)[:, :, :, 2 * u : 2 * u + 2],
+            )
+        codes1, plane1 = quantize_w([w1_pairs[t // 2][:, t % 2] for t in range(PACK)], "1")
 
         picked = keep.tile([P, S], U32, name="picked", tag="grouped1", align_bytes=64)
         for h in range(2):
@@ -104,21 +115,23 @@ def tile_picked_phglu_silu_po_kernel(
                     )
             return bank
 
-        gates = []
-        for b, block in enumerate(blocks):
-            bank = product("1", block, codes1, plane1, HALF)
-            gate = keep.tile([P, block[1], block[3]], F32, name="gate%d" % b, align_bytes=64)
-            nc.scalar.activation(out=gate[:], in_=bank[:], func=SILU)
-            gates.append(gate)
-
         pairs = [keep.tile([P, 2, P, PACK], BF16, name="pair%d" % u, align_bytes=64) for u in range(2)]
         for j in (0, 2):
-            src = raw2[:, j : j + 2, :].rearrange("p j (m e t) -> p m t e j", e=2, t=PACK)
+            src = raw2[j][:].rearrange("p j (m e t) -> p m t e j", e=2, t=PACK)
             for u in range(2):
-                nc.vector.tensor_copy(
+                copy = nc.scalar.copy if (j, u) == (0, 1) else nc.vector.tensor_copy
+                copy(
                     out=pairs[u][:, :, :, j : j + 2].rearrange("p t (m e) j -> p m t e j", e=2),
                     in_=src[:, :, 2 * u : 2 * u + 2],
                 )
+        all_gates = reuse.tile([P, len(blocks), S], F32, name="all_gates", offset=0, align_bytes=64)
+        gates = []
+        for b, block in enumerate(blocks):
+            bank = product("1", block, codes1, plane1, HALF)
+            gate = all_gates[:, b, :].rearrange("p (t c) -> p t c", t=block[1])
+            nc.scalar.activation(out=gate, in_=bank[:], func=SILU)
+            gates.append(gate)
+
         codes2, plane2 = quantize_w([pairs[t // 2][:, t % 2] for t in range(PACK)], "2")
 
         y_rows = out_0.rearrange("(p t) j -> p t j", t=PACK)

@@ -37,21 +37,29 @@ def tile_picked_phglu_silu_po_kernel(
 
         raw1 = keep.tile([P, PACK, N], F32, name="raw1", align_bytes=64)
         w1_rows = w1.rearrange("(p j) c -> p j c", j=PACK)
-        nc.sync.dma_start(out=raw1[:, 0:1, :], in_=w1_rows[:, 0:1, :])
+        nc.sync.dma_start(out=raw1[:, 0:2, :], in_=w1_rows[:, 0:2, :])
         offsets = keep.tile([P, S // 16], U16, name="offsets")
         nc.sync.dma_start(offsets[:], offs)
 
-        scale_table = reuse.tile([P, T], U8, name="scale_table", offset=2 * PAIR_BYTES - T // 2, align_bytes=64)
+        scale_table = reuse.tile([P, T], U8, name="scale_table", offset=2 * PAIR_BYTES, align_bytes=64)
         nc.vector.memset(scale_table[:].bitcast(I32), 0)
         nc.sync.dma_start(out=scale_table[0:P:8, :].bitcast(I32), in_=x_scales[0].bitcast(I32))
 
 
-        nc.sync.dma_start(out=raw1[:, 1:4, :], in_=w1_rows[:, 1:4, :])
+        nc.sync.dma_start(out=raw1[:, 2:4, :], in_=w1_rows[:, 2:4, :])
         word_table = keep.tile([P, T], U32, name="word_table", align_bytes=64)
         nc.sync.dma_start(
             out=word_table[:].bitcast(I32), in_=x_words[0].rearrange("p c r -> p (c r)").bitcast(I32)
         )
 
+        w2_rows = w2.rearrange("(p j) c -> p j c", j=PACK)
+        raw2 = {}
+
+        def load_w2(j):
+            raw2[j] = reuse.tile([P, 2, N], F32, name="raw2_%d" % j, offset=PAIR_BYTES * (1 + j // 2), align_bytes=64)
+            nc.sync.dma_start(out=raw2[j][:], in_=w2_rows[:, j : j + 2, :])
+
+        load_w2(0)
         picked_scales = keep.tile([P, S], U8, name="picked_scales", align_bytes=64)
         nc.vector.tensor_copy(out=picked_scales[:], in_=scale_table[:].indirect(offsets[:]))
         x_plane = keep.tile([P, S], U8, name="x_plane", align_bytes=64)
@@ -61,11 +69,7 @@ def tile_picked_phglu_silu_po_kernel(
                 out=x_plane[32 * quad : 32 * quad + 4, :].bitcast(I32),
                 in_=picked_scales[32 * quad : 32 * quad + 32 : 8, :].bitcast(I32),
             )
-        w2_rows = w2.rearrange("(p j) c -> p j c", j=PACK)
-        raw2 = {}
-        for j in (0, 2):
-            raw2[j] = reuse.tile([P, 2, N], F32, name="raw2_%d" % j, offset=PAIR_BYTES * (1 + j // 2), align_bytes=64)
-            nc.sync.dma_start(out=raw2[j][:], in_=w2_rows[:, j : j + 2, :])
+        load_w2(2)
 
         def quantize_w(grouped, name):
             codes = keep.tile([P, N], U32, name="w_codes" + name, align_bytes=64)
@@ -89,6 +93,18 @@ def tile_picked_phglu_silu_po_kernel(
             )
         codes1, plane1 = quantize_w([w1_pairs[t // 2][:, t % 2] for t in range(PACK)], "1")
 
+        warm_bank = psum.tile([P, S], F32, name="warm_bank", tag="last_bank")
+        for t in range(2):
+            nc.tensor.matmul_mx(
+                out=warm_bank[:],
+                lhsT=codes1[:, t * P : (t + 1) * P].bitcast(FP8X4),
+                lhsT_scale=plane1[:, t * P : (t + 1) * P],
+                rhs=codes1[:].bitcast(FP8X4),
+                rhs_scale=plane1[:],
+                start=True,
+                stop=True,
+            )
+
         picked = keep.tile([P, S], U32, name="picked", tag="grouped1", align_bytes=64)
         for h in range(2):
             nc.vector.tensor_copy(
@@ -100,7 +116,8 @@ def tile_picked_phglu_silu_po_kernel(
 
         def product(name, block, codes, plane, width):
             t0, nt, c0, nc_cols = block
-            bank = psum.tile([P, nt, nc_cols], F32, name="bank%s_%d_%d" % (name, t0, c0))
+            tag = "last_bank" if (name, c0) == ("2", HALF) else "bank%s_%d_%d" % (name, t0, c0)
+            bank = psum.tile([P, nt, nc_cols], F32, name="bank", tag=tag)
             for t in range(t0, t0 + nt):
                 for lo in range(0, nc_cols, width):
                     n = min(width, nc_cols)
@@ -127,7 +144,7 @@ def tile_picked_phglu_silu_po_kernel(
         all_gates = reuse.tile([P, len(blocks), S], F32, name="all_gates", offset=0, align_bytes=64)
         gates = []
         for b, block in enumerate(blocks):
-            bank = product("1", block, codes1, plane1, HALF)
+            bank = product("1", block, codes1, plane1, QUARTER)
             gate = all_gates[:, b, :].rearrange("p (t c) -> p t c", t=block[1])
             nc.scalar.activation(out=gate, in_=bank[:], func=SILU)
             gates.append(gate)

@@ -14,6 +14,7 @@ U8 = mybir.dt.uint8
 FP8X4 = mybir.dt.float8_e4m3fn_x4
 SILU = mybir.ActivationFunctionType.Silu
 MULT = mybir.AluOpType.mult
+ADD = mybir.AluOpType.add
 
 P = 128
 PACK = 4
@@ -41,7 +42,7 @@ def tile_picked_phglu_silu_po_kernel(
         offsets = keep.tile([P, S // 16], U16, name="offsets")
         nc.sync.dma_start(offsets[:], offs)
 
-        scale_table = reuse.tile([P, T], U8, name="scale_table", offset=2 * PAIR_BYTES, align_bytes=64)
+        scale_table = reuse.tile([P, T], U8, name="scale_table", offset=PAIR_BYTES, align_bytes=64)
         nc.vector.memset(scale_table[:].bitcast(I32), 0)
         nc.sync.dma_start(out=scale_table[0:P:8, :].bitcast(I32), in_=x_scales[0].bitcast(I32))
 
@@ -56,7 +57,7 @@ def tile_picked_phglu_silu_po_kernel(
         raw2 = {}
 
         def load_w2(j):
-            raw2[j] = reuse.tile([P, 2, N], F32, name="raw2_%d" % j, offset=PAIR_BYTES * (1 + j // 2), align_bytes=64)
+            raw2[j] = reuse.tile([P, 2, N], F32, name="raw2_%d" % j, offset=PAIR_BYTES * (j // 2), align_bytes=64)
             nc.sync.dma_start(out=raw2[j][:], in_=w2_rows[:, j : j + 2, :])
 
         load_w2(0)
@@ -71,17 +72,11 @@ def tile_picked_phglu_silu_po_kernel(
             )
         load_w2(2)
 
-        def quantize_w(grouped, name):
-            codes = keep.tile([P, N], U32, name="w_codes" + name, align_bytes=64)
-            plane = keep.tile([P, N], U8, name="w_plane" + name, align_bytes=64)
-            for t in range(PACK):
-                cols = slice(t * P, (t + 1) * P)
-                nc.vector.quantize_mx(
-                    out=codes[:, cols].bitcast(FP8X4),
-                    scales=plane[:, cols],
-                    in_=grouped[t].rearrange("p m j -> p (m j)"),
-                )
-            return codes, plane
+        def quantize_w(grouped, codes, plane, t):
+            cols = slice(t * P, (t + 1) * P)
+            nc.vector.quantize_mx(
+                out=codes[:, cols].bitcast(FP8X4), scales=plane[:, cols], in_=grouped.rearrange("p m j -> p (m j)")
+            )
 
         w1_pairs = [
             keep.tile([P, 2, P, PACK], BF16, name="w1_pair", tag=tag, align_bytes=64) for tag in ("w1_pair", "grouped1")
@@ -91,9 +86,12 @@ def tile_picked_phglu_silu_po_kernel(
                 out=w1_pairs[u][:].rearrange("p t m j -> p m j t"),
                 in_=raw1[:].rearrange("p j (m t) -> p m j t", t=PACK)[:, :, :, 2 * u : 2 * u + 2],
             )
-        codes1, plane1 = quantize_w([w1_pairs[t // 2][:, t % 2] for t in range(PACK)], "1")
+        codes1 = keep.tile([P, N], U32, name="w_codes1", align_bytes=64)
+        plane1 = keep.tile([P, N], U8, name="w_plane1", align_bytes=64)
+        for t in range(PACK):
+            quantize_w(w1_pairs[t // 2][:, t % 2], codes1, plane1, t)
 
-        warm_bank = psum.tile([P, S], F32, name="warm_bank", tag="last_bank")
+        warm_bank = psum.tile([P, S], F32, name="warm_bank", tag="bank2_2_0")
         for t in range(2):
             nc.tensor.matmul_mx(
                 out=warm_bank[:],
@@ -116,7 +114,9 @@ def tile_picked_phglu_silu_po_kernel(
 
         def product(name, block, codes, plane, width):
             t0, nt, c0, nc_cols = block
-            tag = "last_bank" if (name, c0) == ("2", HALF) else "bank%s_%d_%d" % (name, t0, c0)
+            tag = "bank%s_%d_%d" % (name, t0, c0)
+            if (name, t0, c0) == ("2", 2, HALF):
+                tag = "bank1_0_0"
             bank = psum.tile([P, nt, nc_cols], F32, name="bank", tag=tag)
             for t in range(t0, t0 + nt):
                 for lo in range(0, nc_cols, width):
@@ -133,15 +133,18 @@ def tile_picked_phglu_silu_po_kernel(
             return bank
 
         pairs = [keep.tile([P, 2, P, PACK], BF16, name="pair%d" % u, align_bytes=64) for u in range(2)]
-        for j in (0, 2):
+
+        def round_w2(copy, j, u, lines):
             src = raw2[j][:].rearrange("p j (m e t) -> p m t e j", e=2, t=PACK)
-            for u in range(2):
-                copy = nc.scalar.copy if (j, u) == (0, 1) else nc.vector.tensor_copy
-                copy(
-                    out=pairs[u][:, :, :, j : j + 2].rearrange("p t (m e) j -> p m t e j", e=2),
-                    in_=src[:, :, 2 * u : 2 * u + 2],
-                )
-        all_gates = reuse.tile([P, len(blocks), S], F32, name="all_gates", offset=0, align_bytes=64)
+            dst = pairs[u][:, :, :, j : j + 2].rearrange("p t (m e) j -> p m t e j", e=2)
+            copy(out=dst[:, lines], in_=src[:, lines, 2 * u : 2 * u + 2])
+
+        round_w2(nc.vector.tensor_copy, 0, 0, slice(0, P // 2))
+        round_w2(nc.scalar.copy, 0, 1, slice(0, P // 2))
+        round_w2(nc.vector.tensor_copy, 2, 0, slice(0, P // 2))
+        round_w2(nc.vector.tensor_copy, 2, 1, slice(0, P // 4))
+        round_w2(nc.scalar.copy, 2, 1, slice(P // 4, P // 2))
+        all_gates = reuse.tile([P, len(blocks), S], F32, name="all_gates", offset=PAIR_BYTES + T, align_bytes=64)
         gates = []
         for b, block in enumerate(blocks):
             bank = product("1", block, codes1, plane1, QUARTER)
@@ -149,7 +152,10 @@ def tile_picked_phglu_silu_po_kernel(
             nc.scalar.activation(out=gate, in_=bank[:], func=SILU)
             gates.append(gate)
 
-        codes2, plane2 = quantize_w([pairs[t // 2][:, t % 2] for t in range(PACK)], "2")
+        codes2 = keep.tile([P, N], U32, name="w_codes2", align_bytes=64)
+        plane2 = keep.tile([P, N], U8, name="w_plane2", align_bytes=64)
+        for t in range(PACK):
+            quantize_w(pairs[t // 2][:, t % 2], codes2, plane2, t)
 
         y_rows = out_0.rearrange("(p t) j -> p t j", t=PACK)
         y_words = out_1[0].rearrange("p c r -> p (c r)").bitcast(I32)
@@ -157,12 +163,16 @@ def tile_picked_phglu_silu_po_kernel(
         y = keep.tile([P, PACK, S], F32, name="y", align_bytes=64)
         for b, block in enumerate(blocks):
             t0, nt, c0, width = block
-            bank = product("2", block, codes2, plane2, S)
-            step = width // nt
+            step = HALF if b == 0 else width // nt
             for lo in range(0, width, step):
+                if b == 0:
+                    bank = product("2", (t0, nt, lo, step), codes2, plane2, S)
+                elif lo == 0:
+                    bank = product("2", block, codes2, plane2, S)
+                first = 0 if b == 0 else lo
                 nc.vector.tensor_tensor(
                     out=y[:, t0 : t0 + nt, c0 + lo : c0 + lo + step],
-                    in0=bank[:, :, lo : lo + step],
+                    in0=bank[:, :, first : first + step],
                     in1=gates[b][:, :, lo : lo + step],
                     op=MULT,
                 )
@@ -177,7 +187,16 @@ def tile_picked_phglu_silu_po_kernel(
                 rounded = keep.tile([P, QUARTER, PACK], BF16, name="rounded%d" % q, align_bytes=64)
                 dst = rounded[:].rearrange("p (c i) t -> p c t i", i=4)
                 src = y[:, :, q * QUARTER : (q + 1) * QUARTER].rearrange("p t (c i) -> p c t i", i=4)
-                if q == 3:
+                if q == 0:
+                    nc.gpsimd.tensor_scalar(
+                        out=rounded[:],
+                        in0=y[:, :, 0:QUARTER].rearrange("p t c -> p c t"),
+                        scalar1=1.0,
+                        scalar2=-0.0,
+                        op0=MULT,
+                        op1=ADD,
+                    )
+                elif q == 3:
                     nc.vector.tensor_copy(out=dst, in_=src)
                 else:
                     nc.scalar.copy(out=dst, in_=src)

@@ -18,9 +18,10 @@ ADD = mybir.AluOpType.add
 
 P = 128
 PACK = 4
-QUARTER = 128
-HALF = 256
+QUARTER = S // 4
+HALF = S // 2
 PAIR_BYTES = 2 * N * 4
+LINES = P // 2
 
 
 def tile_picked_phglu_silu_po_kernel(
@@ -32,26 +33,23 @@ def tile_picked_phglu_silu_po_kernel(
         reuse = ctx.enter_context(tc.tile_pool(name="reuse", bufs=1))
         psum = ctx.enter_context(tc.psum_pool(name="psum", bufs=1))
 
-        warm = keep.tile([P, 2], F32, name="warm")
-        nc.gpsimd.memset(warm[:, 0:1], 0.0)
-        nc.scalar.activation(out=warm[:, 1:2], in_=warm[:, 0:1], func=SILU)
-
         raw1 = keep.tile([P, PACK, N], F32, name="raw1", align_bytes=64)
         w1_rows = w1.rearrange("(p j) c -> p j c", j=PACK)
         nc.sync.dma_start(out=raw1[:, 0:2, :], in_=w1_rows[:, 0:2, :])
         offsets = keep.tile([P, S // 16], U16, name="offsets")
         nc.sync.dma_start(offsets[:], offs)
-
         scale_table = reuse.tile([P, T], U8, name="scale_table", offset=PAIR_BYTES, align_bytes=64)
         nc.vector.memset(scale_table[:].bitcast(I32), 0)
         nc.sync.dma_start(out=scale_table[0:P:8, :].bitcast(I32), in_=x_scales[0].bitcast(I32))
-
-
         nc.sync.dma_start(out=raw1[:, 2:4, :], in_=w1_rows[:, 2:4, :])
         word_table = keep.tile([P, T], U32, name="word_table", align_bytes=64)
         nc.sync.dma_start(
             out=word_table[:].bitcast(I32), in_=x_words[0].rearrange("p c r -> p (c r)").bitcast(I32)
         )
+
+        warm = keep.tile([P, 2], F32, name="warm")
+        nc.vector.memset(warm[:, 0:1], 0.0)
+        nc.scalar.activation(out=warm[:, 1:2], in_=warm[:, 0:1], func=SILU)
 
         w2_rows = w2.rearrange("(p j) c -> p j c", j=PACK)
         raw2 = {}
@@ -72,26 +70,27 @@ def tile_picked_phglu_silu_po_kernel(
             )
         load_w2(2)
 
-        def quantize_w(grouped, codes, plane, t):
-            cols = slice(t * P, (t + 1) * P)
-            nc.vector.quantize_mx(
-                out=codes[:, cols].bitcast(FP8X4), scales=plane[:, cols], in_=grouped.rearrange("p m j -> p (m j)")
-            )
+        def quantize_w(dealt, name):
+            codes = keep.tile([P, N], U32, name="codes" + name, align_bytes=64)
+            plane = keep.tile([P, N], U8, name="plane" + name, align_bytes=64)
+            for t in range(PACK):
+                cols = slice(t * P, (t + 1) * P)
+                nc.vector.quantize_mx(
+                    out=codes[:, cols].bitcast(FP8X4),
+                    scales=plane[:, cols],
+                    in_=dealt[t // 2][:, t % 2].rearrange("p m j -> p (m j)"),
+                )
+            return codes, plane
 
-        w1_pairs = [
-            keep.tile([P, 2, P, PACK], BF16, name="w1_pair", tag=tag, align_bytes=64) for tag in ("w1_pair", "grouped1")
-        ]
+        dealt1 = [keep.tile([P, 2, P, PACK], BF16, name="dealt1", tag="dealt1_%d" % u, align_bytes=64) for u in range(2)]
         for u, copy in enumerate((nc.vector.tensor_copy, nc.scalar.copy)):
             copy(
-                out=w1_pairs[u][:].rearrange("p t m j -> p m j t"),
+                out=dealt1[u][:].rearrange("p t m j -> p m j t"),
                 in_=raw1[:].rearrange("p j (m t) -> p m j t", t=PACK)[:, :, :, 2 * u : 2 * u + 2],
             )
-        codes1 = keep.tile([P, N], U32, name="w_codes1", align_bytes=64)
-        plane1 = keep.tile([P, N], U8, name="w_plane1", align_bytes=64)
-        for t in range(PACK):
-            quantize_w(w1_pairs[t // 2][:, t % 2], codes1, plane1, t)
+        codes1, plane1 = quantize_w(dealt1, "1")
 
-        warm_bank = psum.tile([P, S], F32, name="warm_bank", tag="bank2_2_0")
+        warm_bank = psum.tile([P, S], F32, name="warm_bank", tag="value_2_0")
         for t in range(2):
             nc.tensor.matmul_mx(
                 out=warm_bank[:],
@@ -103,106 +102,107 @@ def tile_picked_phglu_silu_po_kernel(
                 stop=True,
             )
 
-        picked = keep.tile([P, S], U32, name="picked", tag="grouped1", align_bytes=64)
+        picked = keep.tile([P, S], U32, name="picked", tag="dealt1_1", align_bytes=64)
         for h in range(2):
             nc.vector.tensor_copy(
                 out=picked[:, h * HALF : (h + 1) * HALF],
                 in_=word_table[:].indirect(offsets[:, h * HALF // 16 : (h + 1) * HALF // 16]),
             )
 
-        blocks = ((0, 1, 0, S), (1, 1, 0, S), (2, 2, 0, HALF), (2, 2, HALF, HALF))
-
-        def product(name, block, codes, plane, width):
-            t0, nt, c0, nc_cols = block
-            tag = "bank%s_%d_%d" % (name, t0, c0)
-            if (name, t0, c0) == ("2", 2, HALF):
-                tag = "bank1_0_0"
-            bank = psum.tile([P, nt, nc_cols], F32, name="bank", tag=tag)
-            for t in range(t0, t0 + nt):
-                for lo in range(0, nc_cols, width):
-                    n = min(width, nc_cols)
+        def product(tag, codes, plane, t0, groups, c0, width, step):
+            bank = psum.tile([P, groups, width], F32, name="bank", tag=tag)
+            for t in range(t0, t0 + groups):
+                for lo in range(0, width, step):
                     nc.tensor.matmul_mx(
-                        out=bank[:, t - t0, lo : lo + n],
+                        out=bank[:, t - t0, lo : lo + step],
                         lhsT=codes[:, t * P : (t + 1) * P].bitcast(FP8X4),
                         lhsT_scale=plane[:, t * P : (t + 1) * P],
-                        rhs=picked[:, c0 + lo : c0 + lo + n].bitcast(FP8X4),
-                        rhs_scale=x_plane[:, c0 + lo : c0 + lo + n],
+                        rhs=picked[:, c0 + lo : c0 + lo + step].bitcast(FP8X4),
+                        rhs_scale=x_plane[:, c0 + lo : c0 + lo + step],
                         start=True,
                         stop=True,
                     )
             return bank
 
-        pairs = [keep.tile([P, 2, P, PACK], BF16, name="pair%d" % u, align_bytes=64) for u in range(2)]
+        dealt2 = [keep.tile([P, 2, P, PACK], BF16, name="dealt2_%d" % u, align_bytes=64) for u in range(2)]
 
         def round_w2(copy, j, u, lines):
             src = raw2[j][:].rearrange("p j (m e t) -> p m t e j", e=2, t=PACK)
-            dst = pairs[u][:, :, :, j : j + 2].rearrange("p t (m e) j -> p m t e j", e=2)
+            dst = dealt2[u][:, :, :, j : j + 2].rearrange("p t (m e) j -> p m t e j", e=2)
             copy(out=dst[:, lines], in_=src[:, lines, 2 * u : 2 * u + 2])
 
-        round_w2(nc.vector.tensor_copy, 0, 0, slice(0, P // 2))
-        round_w2(nc.scalar.copy, 0, 1, slice(0, P // 2))
-        round_w2(nc.vector.tensor_copy, 2, 0, slice(0, P // 2))
-        round_w2(nc.vector.tensor_copy, 2, 1, slice(0, P // 4))
-        round_w2(nc.scalar.copy, 2, 1, slice(P // 4, P // 2))
-        all_gates = reuse.tile([P, len(blocks), S], F32, name="all_gates", offset=PAIR_BYTES + T, align_bytes=64)
-        gates = []
-        for b, block in enumerate(blocks):
-            bank = product("1", block, codes1, plane1, QUARTER)
-            gate = all_gates[:, b, :].rearrange("p (t c) -> p t c", t=block[1])
-            nc.scalar.activation(out=gate, in_=bank[:], func=SILU)
-            gates.append(gate)
+        round_w2(nc.vector.tensor_copy, 0, 0, slice(0, LINES))
+        round_w2(nc.scalar.copy, 0, 1, slice(0, LINES))
+        round_w2(nc.vector.tensor_copy, 2, 0, slice(0, LINES))
+        round_w2(nc.vector.tensor_copy, 2, 1, slice(0, LINES // 2))
 
-        codes2 = keep.tile([P, N], U32, name="w_codes2", align_bytes=64)
-        plane2 = keep.tile([P, N], U8, name="w_plane2", align_bytes=64)
-        for t in range(PACK):
-            quantize_w(pairs[t // 2][:, t % 2], codes2, plane2, t)
+        sections = ((0, 1, 0, S), (1, 1, 0, S), (2, 2, 0, HALF), (2, 2, HALF, HALF))
+
+        first_gate = reuse.tile([P, S], F32, name="first_gate", offset=0, align_bytes=64)
+        later_gates = reuse.tile([P, 3, S], F32, name="later_gates", offset=PAIR_BYTES + T, align_bytes=64)
+        gates = []
+        for s, (t0, groups, c0, width) in enumerate(sections):
+            bank = product("gate_%d_%d" % (t0, c0), codes1, plane1, t0, groups, c0, width, QUARTER)
+            gate = (later_gates[:, s - 1, :] if s else first_gate[:]).rearrange("p (t c) -> p t c", t=groups)
+            step = HALF if s == 0 else width
+            for lo in range(0, width, step):
+                nc.scalar.activation(out=gate[:, :, lo : lo + step], in_=bank[:, :, lo : lo + step], func=SILU)
+            gates.append(gate)
+            if s == 0:
+                round_w2(nc.scalar.copy, 2, 1, slice(LINES // 2, LINES))
+
+        codes2, plane2 = quantize_w(dealt2, "2")
 
         y_rows = out_0.rearrange("(p t) j -> p t j", t=PACK)
+        y = keep.tile([P, PACK, S], F32, name="y", align_bytes=64)
+
+        def gate_product(bank, s, lo, hi):
+            t0, groups, c0, width = sections[s]
+            nc.vector.tensor_tensor(
+                out=y[:, t0 : t0 + groups, c0 + lo : c0 + hi], in0=bank, in1=gates[s][:, :, lo:hi], op=MULT
+            )
+
+        for s, (t0, groups, c0, width) in enumerate(sections):
+            if s == 0:
+                for lo in (0, HALF):
+                    bank = product("value_0_%d" % lo, codes2, plane2, t0, groups, lo, HALF, HALF)
+                    gate_product(bank[:], s, lo, lo + HALF)
+            else:
+                tag = "gate_0_0" if s == len(sections) - 1 else "value_%d_%d" % (t0, c0)
+                bank = product(tag, codes2, plane2, t0, groups, c0, width, width)
+                step = width // groups
+                for lo in range(0, width, step):
+                    gate_product(bank[:, :, lo : lo + step], s, lo, lo + step)
+            nc.sync.dma_start(
+                out=y_rows[:, t0 : t0 + groups, c0 : c0 + width], in_=y[:, t0 : t0 + groups, c0 : c0 + width]
+            )
+
         y_words = out_1[0].rearrange("p c r -> p (c r)").bitcast(I32)
         y_plane = keep.tile([P, S], U8, name="y_plane", align_bytes=64)
-        y = keep.tile([P, PACK, S], F32, name="y", align_bytes=64)
-        for b, block in enumerate(blocks):
-            t0, nt, c0, width = block
-            step = HALF if b == 0 else width // nt
-            for lo in range(0, width, step):
-                if b == 0:
-                    bank = product("2", (t0, nt, lo, step), codes2, plane2, S)
-                elif lo == 0:
-                    bank = product("2", block, codes2, plane2, S)
-                first = 0 if b == 0 else lo
-                nc.vector.tensor_tensor(
-                    out=y[:, t0 : t0 + nt, c0 + lo : c0 + lo + step],
-                    in0=bank[:, :, first : first + step],
-                    in1=gates[b][:, :, lo : lo + step],
-                    op=MULT,
-                )
-            nc.sync.dma_start(
-                out=y_rows[:, t0 : t0 + nt, c0 : c0 + width], in_=y[:, t0 : t0 + nt, c0 : c0 + width]
-            )
         for h in range(2):
             y_codes = keep.tile([P, HALF], U32, name="y_codes%d" % h, align_bytes=64)
             for u in range(2):
                 q = 2 * h + u
-                cols = slice(u * QUARTER, (u + 1) * QUARTER)
+                places = slice(q * QUARTER, (q + 1) * QUARTER)
                 rounded = keep.tile([P, QUARTER, PACK], BF16, name="rounded%d" % q, align_bytes=64)
-                dst = rounded[:].rearrange("p (c i) t -> p c t i", i=4)
-                src = y[:, :, q * QUARTER : (q + 1) * QUARTER].rearrange("p t (c i) -> p c t i", i=4)
                 if q == 0:
                     nc.gpsimd.tensor_scalar(
                         out=rounded[:],
-                        in0=y[:, :, 0:QUARTER].rearrange("p t c -> p c t"),
+                        in0=y[:, :, places].rearrange("p t c -> p c t"),
                         scalar1=1.0,
                         scalar2=-0.0,
                         op0=MULT,
                         op1=ADD,
                     )
-                elif q == 3:
-                    nc.vector.tensor_copy(out=dst, in_=src)
                 else:
-                    nc.scalar.copy(out=dst, in_=src)
+                    copy = nc.vector.tensor_copy if q == 3 else nc.scalar.copy
+                    copy(
+                        out=rounded[:].rearrange("p (c i) t -> p c t i", i=4),
+                        in_=y[:, :, places].rearrange("p t (c i) -> p c t i", i=4),
+                    )
                 nc.vector.quantize_mx(
-                    out=y_codes[:, cols].bitcast(FP8X4),
-                    scales=y_plane[:, q * QUARTER : (q + 1) * QUARTER],
+                    out=y_codes[:, u * QUARTER : (u + 1) * QUARTER].bitcast(FP8X4),
+                    scales=y_plane[:, places],
                     in_=rounded[:].rearrange("p c t -> p (c t)"),
                 )
             nc.sync.dma_start(out=y_words[:, h * HALF : (h + 1) * HALF], in_=y_codes[:].bitcast(I32))

@@ -55,8 +55,8 @@ def tile_picked_phglu_silu_po_kernel(
         raw2 = {}
 
         def load_w2(j):
-            raw2[j] = reuse.tile([P, 2, N], F32, name="raw2_%d" % j, offset=PAIR_BYTES * (j // 2), align_bytes=64)
-            nc.sync.dma_start(out=raw2[j][:], in_=w2_rows[:, j : j + 2, :])
+            raw2[j] = reuse.tile([P, PACK, N // 2], F32, name="raw2_%d" % j, offset=PAIR_BYTES * j, align_bytes=64)
+            nc.sync.dma_start(out=raw2[j][:], in_=w2_rows[:, :, j * N // 2 : (j + 1) * N // 2])
 
         load_w2(0)
         picked_scales = keep.tile([P, S], U8, name="picked_scales", align_bytes=64)
@@ -68,7 +68,7 @@ def tile_picked_phglu_silu_po_kernel(
                 out=x_plane[32 * quad : 32 * quad + 4, :].bitcast(I32),
                 in_=picked_scales[32 * quad : 32 * quad + 32 : 8, :].bitcast(I32),
             )
-        load_w2(2)
+        load_w2(1)
 
         def quantize_w(dealt, name):
             codes = keep.tile([P, N], U32, name="codes" + name, align_bytes=64)
@@ -90,7 +90,7 @@ def tile_picked_phglu_silu_po_kernel(
             )
         codes1, plane1 = quantize_w(dealt1, "1")
 
-        warm_bank = psum.tile([P, S], F32, name="warm_bank", tag="value_2_0")
+        warm_bank = psum.tile([P, S], F32, name="warm_bank", tag="value_1_0")
         for t in range(2):
             nc.tensor.matmul_mx(
                 out=warm_bank[:],
@@ -124,17 +124,30 @@ def tile_picked_phglu_silu_po_kernel(
                     )
             return bank
 
-        dealt2 = [keep.tile([P, 2, P, PACK], BF16, name="dealt2_%d" % u, align_bytes=64) for u in range(2)]
+        codes2 = keep.tile([P, N], U32, name="codes2", align_bytes=64)
+        plane2 = keep.tile([P, N], U8, name="plane2", align_bytes=64)
+        dealt2 = {}
 
-        def round_w2(copy, j, u, lines):
-            src = raw2[j][:].rearrange("p j (m e t) -> p m t e j", e=2, t=PACK)
-            dst = dealt2[u][:, :, :, j : j + 2].rearrange("p t (m e) j -> p m t e j", e=2)
-            copy(out=dst[:, lines], in_=src[:, lines, 2 * u : 2 * u + 2])
+        def round_w2(copy, h, u):
+            dealt2[h, u] = keep.tile([P, 2, LINES, PACK], BF16, name="dealt2_%d_%d" % (h, u), align_bytes=64)
+            copy(
+                out=dealt2[h, u][:].rearrange("p t m j -> p m j t"),
+                in_=raw2[h][:].rearrange("p j (m t) -> p m j t", t=PACK)[:, :, :, 2 * u : 2 * u + 2],
+            )
 
-        round_w2(nc.vector.tensor_copy, 0, 0, slice(0, LINES))
-        round_w2(nc.scalar.copy, 0, 1, slice(0, LINES))
-        round_w2(nc.vector.tensor_copy, 2, 0, slice(0, LINES))
-        round_w2(nc.vector.tensor_copy, 2, 1, slice(0, LINES // 2))
+        def quantize_w2(h):
+            for t in range(PACK):
+                cols = slice(t * P + h * LINES, t * P + (h + 1) * LINES)
+                nc.vector.quantize_mx(
+                    out=codes2[:, cols].bitcast(FP8X4),
+                    scales=plane2[:, cols],
+                    in_=dealt2[h, t // 2][:, t % 2].rearrange("p m j -> p (m j)"),
+                )
+
+        round_w2(nc.vector.tensor_copy, 0, 0)
+        round_w2(nc.scalar.copy, 0, 1)
+        quantize_w2(0)
+        round_w2(nc.vector.tensor_copy, 1, 0)
 
         sections = ((0, 1, 0, S), (1, 1, 0, S), (2, 2, 0, HALF), (2, 2, HALF, HALF))
 
@@ -142,24 +155,25 @@ def tile_picked_phglu_silu_po_kernel(
         later_gates = reuse.tile([P, 3, S], F32, name="later_gates", offset=PAIR_BYTES + T, align_bytes=64)
         gates = []
         for s, (t0, groups, c0, width) in enumerate(sections):
-            bank = product("gate_%d_%d" % (t0, c0), codes1, plane1, t0, groups, c0, width, QUARTER)
             gate = (later_gates[:, s - 1, :] if s else first_gate[:]).rearrange("p (t c) -> p t c", t=groups)
             step = HALF if s == 0 else width
             for lo in range(0, width, step):
-                nc.scalar.activation(out=gate[:, :, lo : lo + step], in_=bank[:, :, lo : lo + step], func=SILU)
+                tag = "gate_%d_%d" % (t0, c0 + lo)
+                bank = product(tag, codes1, plane1, t0, groups, c0 + lo, step, QUARTER if s else HALF)
+                nc.scalar.activation(out=gate[:, :, lo : lo + step], in_=bank[:], func=SILU)
             gates.append(gate)
             if s == 0:
-                round_w2(nc.scalar.copy, 2, 1, slice(LINES // 2, LINES))
+                round_w2(nc.scalar.copy, 1, 1)
 
-        codes2, plane2 = quantize_w(dealt2, "2")
+        quantize_w2(1)
 
         y_rows = out_0.rearrange("(p t) j -> p t j", t=PACK)
         y = keep.tile([P, PACK, S], F32, name="y", align_bytes=64)
 
-        def gate_product(bank, s, lo, hi):
+        def gate_product(bank, s, lo, hi, part=slice(None)):
             t0, groups, c0, width = sections[s]
             nc.vector.tensor_tensor(
-                out=y[:, t0 : t0 + groups, c0 + lo : c0 + hi], in0=bank, in1=gates[s][:, :, lo:hi], op=MULT
+                out=y[:, t0 : t0 + groups, c0 + lo : c0 + hi][:, part], in0=bank, in1=gates[s][:, part, lo:hi], op=MULT
             )
 
         for s, (t0, groups, c0, width) in enumerate(sections):
@@ -168,14 +182,20 @@ def tile_picked_phglu_silu_po_kernel(
                     bank = product("value_0_%d" % lo, codes2, plane2, t0, groups, lo, HALF, HALF)
                     gate_product(bank[:], s, lo, lo + HALF)
             else:
-                tag = "gate_0_0" if s == len(sections) - 1 else "value_%d_%d" % (t0, c0)
+                tag = ("value_1_0", "gate_0_0", "gate_0_256")[s - 1]
                 bank = product(tag, codes2, plane2, t0, groups, c0, width, width)
+                if s == len(sections) - 1:
+                    gate_product(bank[:, 0:1, :], s, 0, width, slice(0, 1))
+                    nc.sync.dma_start(out=y_rows[:, 2, :], in_=y[:, 2, :])
+                    for lo in (0, QUARTER):
+                        gate_product(bank[:, 1:2, lo : lo + QUARTER], s, lo, lo + QUARTER, slice(1, 2))
+                    nc.sync.dma_start(out=y_rows[:, 3, :], in_=y[:, 3, :])
+                    continue
                 step = width // groups
                 for lo in range(0, width, step):
                     gate_product(bank[:, :, lo : lo + step], s, lo, lo + step)
-            nc.sync.dma_start(
-                out=y_rows[:, t0 : t0 + groups, c0 : c0 + width], in_=y[:, t0 : t0 + groups, c0 : c0 + width]
-            )
+            if groups == 1:
+                nc.sync.dma_start(out=y_rows[:, t0, :], in_=y[:, t0, :])
 
         y_words = out_1[0].rearrange("p c r -> p (c r)").bitcast(I32)
         y_plane = keep.tile([P, S], U8, name="y_plane", align_bytes=64)

@@ -48,7 +48,7 @@ def tile_picked_phglu_silu_po_kernel(
         )
 
         warm = keep.tile([P, 2], F32, name="warm")
-        nc.vector.memset(warm[:, 0:1], 0.0)
+        nc.gpsimd.memset(warm[:, 0:1], 0.0)
         nc.scalar.activation(out=warm[:, 1:2], in_=warm[:, 0:1], func=SILU)
 
         w2_rows = w2.rearrange("(p j) c -> p j c", j=PACK)
@@ -73,12 +73,12 @@ def tile_picked_phglu_silu_po_kernel(
         def quantize_w(dealt, name):
             codes = keep.tile([P, N], U32, name="codes" + name, align_bytes=64)
             plane = keep.tile([P, N], U8, name="plane" + name, align_bytes=64)
-            for t in range(PACK):
-                cols = slice(t * P, (t + 1) * P)
+            for u in range(2):
+                cols = slice(2 * u * P, 2 * (u + 1) * P)
                 nc.vector.quantize_mx(
                     out=codes[:, cols].bitcast(FP8X4),
                     scales=plane[:, cols],
-                    in_=dealt[t // 2][:, t % 2].rearrange("p m j -> p (m j)"),
+                    in_=dealt[u][:].rearrange("p t m j -> p (t m j)"),
                 )
             return codes, plane
 
@@ -128,11 +128,12 @@ def tile_picked_phglu_silu_po_kernel(
         plane2 = keep.tile([P, N], U8, name="plane2", align_bytes=64)
         dealt2 = {}
 
-        def round_w2(copy, h, u):
-            dealt2[h, u] = keep.tile([P, 2, LINES, PACK], BF16, name="dealt2_%d_%d" % (h, u), align_bytes=64)
+        def round_w2(copy, h, u, part=slice(0, LINES)):
+            if (h, u) not in dealt2:
+                dealt2[h, u] = keep.tile([P, 2, LINES, PACK], BF16, name="dealt2_%d_%d" % (h, u), align_bytes=64)
             copy(
-                out=dealt2[h, u][:].rearrange("p t m j -> p m j t"),
-                in_=raw2[h][:].rearrange("p j (m t) -> p m j t", t=PACK)[:, :, :, 2 * u : 2 * u + 2],
+                out=dealt2[h, u][:, :, part].rearrange("p t m j -> p m j t"),
+                in_=raw2[h][:].rearrange("p j (m t) -> p m j t", t=PACK)[:, part, :, 2 * u : 2 * u + 2],
             )
 
         def quantize_w2(h):
@@ -148,6 +149,7 @@ def tile_picked_phglu_silu_po_kernel(
         round_w2(nc.scalar.copy, 0, 1)
         quantize_w2(0)
         round_w2(nc.vector.tensor_copy, 1, 0)
+        round_w2(nc.vector.tensor_copy, 1, 1, slice(0, LINES // 2))
 
         sections = ((0, 1, 0, S), (1, 1, 0, S), (2, 2, 0, HALF), (2, 2, HALF, HALF))
 
@@ -163,7 +165,7 @@ def tile_picked_phglu_silu_po_kernel(
                 nc.scalar.activation(out=gate[:, :, lo : lo + step], in_=bank[:], func=SILU)
             gates.append(gate)
             if s == 0:
-                round_w2(nc.scalar.copy, 1, 1)
+                round_w2(nc.scalar.copy, 1, 1, slice(LINES // 2, LINES))
 
         quantize_w2(1)
 
@@ -201,13 +203,14 @@ def tile_picked_phglu_silu_po_kernel(
         y_plane = keep.tile([P, S], U8, name="y_plane", align_bytes=64)
         for h in range(2):
             y_codes = keep.tile([P, HALF], U32, name="y_codes%d" % h, align_bytes=64)
+            rounded = keep.tile([P, HALF, PACK], BF16, name="rounded%d" % h, align_bytes=64)
             for u in range(2):
                 q = 2 * h + u
                 places = slice(q * QUARTER, (q + 1) * QUARTER)
-                rounded = keep.tile([P, QUARTER, PACK], BF16, name="rounded%d" % q, align_bytes=64)
+                part = rounded[:, u * QUARTER : (u + 1) * QUARTER, :]
                 if q == 0:
                     nc.gpsimd.tensor_scalar(
-                        out=rounded[:],
+                        out=part,
                         in0=y[:, :, places].rearrange("p t c -> p c t"),
                         scalar1=1.0,
                         scalar2=-0.0,
@@ -217,14 +220,14 @@ def tile_picked_phglu_silu_po_kernel(
                 else:
                     copy = nc.vector.tensor_copy if q == 3 else nc.scalar.copy
                     copy(
-                        out=rounded[:].rearrange("p (c i) t -> p c t i", i=4),
+                        out=part.rearrange("p (c i) t -> p c t i", i=4),
                         in_=y[:, :, places].rearrange("p t (c i) -> p c t i", i=4),
                     )
-                nc.vector.quantize_mx(
-                    out=y_codes[:, u * QUARTER : (u + 1) * QUARTER].bitcast(FP8X4),
-                    scales=y_plane[:, places],
-                    in_=rounded[:].rearrange("p c t -> p (c t)"),
-                )
+            nc.vector.quantize_mx(
+                out=y_codes[:].bitcast(FP8X4),
+                scales=y_plane[:, h * HALF : (h + 1) * HALF],
+                in_=rounded[:].rearrange("p c t -> p (c t)"),
+            )
             nc.sync.dma_start(out=y_words[:, h * HALF : (h + 1) * HALF], in_=y_codes[:].bitcast(I32))
         for quad in range(4):
             queue = nc.sync if quad % 2 == 0 else nc.scalar

@@ -20,8 +20,8 @@ P = 128
 PACK = 4
 QUARTER = S // 4
 HALF = S // 2
-PAIR_BYTES = 2 * N * 4
-LINES = P // 2
+HALF_W_BYTES = PACK * (N // 2) * 4
+HALF_GROUP = P // 2
 
 
 def tile_picked_phglu_silu_po_kernel(
@@ -38,7 +38,7 @@ def tile_picked_phglu_silu_po_kernel(
         nc.sync.dma_start(out=raw1[:, 0:2, :], in_=w1_rows[:, 0:2, :])
         offsets = keep.tile([P, S // 16], U16, name="offsets")
         nc.sync.dma_start(offsets[:], offs)
-        scale_table = reuse.tile([P, T], U8, name="scale_table", offset=PAIR_BYTES, align_bytes=64)
+        scale_table = reuse.tile([P, T], U8, name="scale_table", offset=HALF_W_BYTES, align_bytes=64)
         nc.vector.memset(scale_table[:].bitcast(I32), 0)
         nc.sync.dma_start(out=scale_table[0:P:8, :].bitcast(I32), in_=x_scales[0].bitcast(I32))
         nc.sync.dma_start(out=raw1[:, 2:4, :], in_=w1_rows[:, 2:4, :])
@@ -48,15 +48,15 @@ def tile_picked_phglu_silu_po_kernel(
         )
 
         warm = keep.tile([P, 2], F32, name="warm")
-        nc.gpsimd.memset(warm[:, 0:1], 0.0)
+        nc.vector.memset(warm[:, 0:1], 0.0)
         nc.scalar.activation(out=warm[:, 1:2], in_=warm[:, 0:1], func=SILU)
 
         w2_rows = w2.rearrange("(p j) c -> p j c", j=PACK)
         raw2 = {}
 
-        def load_w2(j):
-            raw2[j] = reuse.tile([P, PACK, N // 2], F32, name="raw2_%d" % j, offset=PAIR_BYTES * j, align_bytes=64)
-            nc.sync.dma_start(out=raw2[j][:], in_=w2_rows[:, :, j * N // 2 : (j + 1) * N // 2])
+        def load_w2(c):
+            raw2[c] = reuse.tile([P, PACK, N // 2], F32, name="raw2_%d" % c, offset=HALF_W_BYTES * c, align_bytes=64)
+            nc.sync.dma_start(out=raw2[c][:], in_=w2_rows[:, :, c * N // 2 : (c + 1) * N // 2])
 
         load_w2(0)
         picked_scales = keep.tile([P, S], U8, name="picked_scales", align_bytes=64)
@@ -70,25 +70,21 @@ def tile_picked_phglu_silu_po_kernel(
             )
         load_w2(1)
 
-        def quantize_w(dealt, name):
-            codes = keep.tile([P, N], U32, name="codes" + name, align_bytes=64)
-            plane = keep.tile([P, N], U8, name="plane" + name, align_bytes=64)
-            for u in range(2):
-                cols = slice(2 * u * P, 2 * (u + 1) * P)
-                nc.vector.quantize_mx(
-                    out=codes[:, cols].bitcast(FP8X4),
-                    scales=plane[:, cols],
-                    in_=dealt[u][:].rearrange("p t m j -> p (t m j)"),
-                )
-            return codes, plane
-
         dealt1 = [keep.tile([P, 2, P, PACK], BF16, name="dealt1", tag="dealt1_%d" % u, align_bytes=64) for u in range(2)]
         for u, copy in enumerate((nc.vector.tensor_copy, nc.scalar.copy)):
             copy(
                 out=dealt1[u][:].rearrange("p t m j -> p m j t"),
                 in_=raw1[:].rearrange("p j (m t) -> p m j t", t=PACK)[:, :, :, 2 * u : 2 * u + 2],
             )
-        codes1, plane1 = quantize_w(dealt1, "1")
+        codes1 = keep.tile([P, N], U32, name="codes1", align_bytes=64)
+        plane1 = keep.tile([P, N], U8, name="plane1", align_bytes=64)
+        for u in range(2):
+            cols = slice(2 * u * P, 2 * (u + 1) * P)
+            nc.vector.quantize_mx(
+                out=codes1[:, cols].bitcast(FP8X4),
+                scales=plane1[:, cols],
+                in_=dealt1[u][:].rearrange("p t m j -> p (t m j)"),
+            )
 
         warm_bank = psum.tile([P, S], F32, name="warm_bank", tag="value_1_0")
         for t in range(2):
@@ -128,33 +124,33 @@ def tile_picked_phglu_silu_po_kernel(
         plane2 = keep.tile([P, N], U8, name="plane2", align_bytes=64)
         dealt2 = {}
 
-        def round_w2(copy, h, u, part=slice(0, LINES)):
-            if (h, u) not in dealt2:
-                dealt2[h, u] = keep.tile([P, 2, LINES, PACK], BF16, name="dealt2_%d_%d" % (h, u), align_bytes=64)
+        def round_w2(copy, c, u, part=slice(0, HALF_GROUP)):
+            if (c, u) not in dealt2:
+                dealt2[c, u] = keep.tile([P, 2, HALF_GROUP, PACK], BF16, name="dealt2_%d_%d" % (c, u), align_bytes=64)
             copy(
-                out=dealt2[h, u][:, :, part].rearrange("p t m j -> p m j t"),
-                in_=raw2[h][:].rearrange("p j (m t) -> p m j t", t=PACK)[:, part, :, 2 * u : 2 * u + 2],
+                out=dealt2[c, u][:, :, part].rearrange("p t m j -> p m j t"),
+                in_=raw2[c][:].rearrange("p j (m t) -> p m j t", t=PACK)[:, part, :, 2 * u : 2 * u + 2],
             )
 
-        def quantize_w2(h):
+        def quantize_w2(c):
             for t in range(PACK):
-                cols = slice(t * P + h * LINES, t * P + (h + 1) * LINES)
+                cols = slice(t * P + c * HALF_GROUP, t * P + (c + 1) * HALF_GROUP)
                 nc.vector.quantize_mx(
                     out=codes2[:, cols].bitcast(FP8X4),
                     scales=plane2[:, cols],
-                    in_=dealt2[h, t // 2][:, t % 2].rearrange("p m j -> p (m j)"),
+                    in_=dealt2[c, t // 2][:, t % 2].rearrange("p m j -> p (m j)"),
                 )
 
         round_w2(nc.vector.tensor_copy, 0, 0)
         round_w2(nc.scalar.copy, 0, 1)
         quantize_w2(0)
         round_w2(nc.vector.tensor_copy, 1, 0)
-        round_w2(nc.vector.tensor_copy, 1, 1, slice(0, LINES // 2))
+        round_w2(nc.vector.tensor_copy, 1, 1, slice(0, HALF_GROUP // 2))
 
         sections = ((0, 1, 0, S), (1, 1, 0, S), (2, 2, 0, HALF), (2, 2, HALF, HALF))
 
         first_gate = reuse.tile([P, S], F32, name="first_gate", offset=0, align_bytes=64)
-        later_gates = reuse.tile([P, 3, S], F32, name="later_gates", offset=PAIR_BYTES + T, align_bytes=64)
+        later_gates = reuse.tile([P, 3, S], F32, name="later_gates", offset=HALF_W_BYTES + T, align_bytes=64)
         gates = []
         for s, (t0, groups, c0, width) in enumerate(sections):
             gate = (later_gates[:, s - 1, :] if s else first_gate[:]).rearrange("p (t c) -> p t c", t=groups)
@@ -165,17 +161,17 @@ def tile_picked_phglu_silu_po_kernel(
                 nc.scalar.activation(out=gate[:, :, lo : lo + step], in_=bank[:], func=SILU)
             gates.append(gate)
             if s == 0:
-                round_w2(nc.scalar.copy, 1, 1, slice(LINES // 2, LINES))
+                round_w2(nc.scalar.copy, 1, 1, slice(HALF_GROUP // 2, HALF_GROUP))
 
         quantize_w2(1)
 
         y_rows = out_0.rearrange("(p t) j -> p t j", t=PACK)
         y = keep.tile([P, PACK, S], F32, name="y", align_bytes=64)
 
-        def gate_product(bank, s, lo, hi, part=slice(None)):
+        def gate_product(bank, s, lo, hi):
             t0, groups, c0, width = sections[s]
             nc.vector.tensor_tensor(
-                out=y[:, t0 : t0 + groups, c0 + lo : c0 + hi][:, part], in0=bank, in1=gates[s][:, part, lo:hi], op=MULT
+                out=y[:, t0 : t0 + groups, c0 + lo : c0 + hi], in0=bank, in1=gates[s][:, :, lo:hi], op=MULT
             )
 
         for s, (t0, groups, c0, width) in enumerate(sections):
@@ -186,18 +182,12 @@ def tile_picked_phglu_silu_po_kernel(
             else:
                 tag = ("value_1_0", "gate_0_0", "gate_0_256")[s - 1]
                 bank = product(tag, codes2, plane2, t0, groups, c0, width, width)
-                if s == len(sections) - 1:
-                    gate_product(bank[:, 0:1, :], s, 0, width, slice(0, 1))
-                    nc.sync.dma_start(out=y_rows[:, 2, :], in_=y[:, 2, :])
-                    for lo in (0, QUARTER):
-                        gate_product(bank[:, 1:2, lo : lo + QUARTER], s, lo, lo + QUARTER, slice(1, 2))
-                    nc.sync.dma_start(out=y_rows[:, 3, :], in_=y[:, 3, :])
-                    continue
                 step = width // groups
                 for lo in range(0, width, step):
                     gate_product(bank[:, :, lo : lo + step], s, lo, lo + step)
-            if groups == 1:
-                nc.sync.dma_start(out=y_rows[:, t0, :], in_=y[:, t0, :])
+            nc.sync.dma_start(
+                out=y_rows[:, t0 : t0 + groups, c0 : c0 + width], in_=y[:, t0 : t0 + groups, c0 : c0 + width]
+            )
 
         y_words = out_1[0].rearrange("p c r -> p (c r)").bitcast(I32)
         y_plane = keep.tile([P, S], U8, name="y_plane", align_bytes=64)
@@ -223,11 +213,13 @@ def tile_picked_phglu_silu_po_kernel(
                         out=part.rearrange("p (c i) t -> p c t i", i=4),
                         in_=y[:, :, places].rearrange("p t (c i) -> p c t i", i=4),
                     )
-            nc.vector.quantize_mx(
-                out=y_codes[:].bitcast(FP8X4),
-                scales=y_plane[:, h * HALF : (h + 1) * HALF],
-                in_=rounded[:].rearrange("p c t -> p (c t)"),
-            )
+            step = QUARTER if h else HALF
+            for lo in range(0, HALF, step):
+                nc.vector.quantize_mx(
+                    out=y_codes[:, lo : lo + step].bitcast(FP8X4),
+                    scales=y_plane[:, h * HALF + lo : h * HALF + lo + step],
+                    in_=rounded[:, lo : lo + step, :].rearrange("p c t -> p (c t)"),
+                )
             nc.sync.dma_start(out=y_words[:, h * HALF : (h + 1) * HALF], in_=y_codes[:].bitcast(I32))
         for quad in range(4):
             queue = nc.sync if quad % 2 == 0 else nc.scalar

@@ -86,12 +86,12 @@ def tile_picked_phglu_silu_po_kernel(
                 in_=dealt1[u][:].rearrange("p t m j -> p (t m j)"),
             )
 
-        warm_bank = psum.tile([P, S], F32, name="warm_bank", tag="value_1_0")
-        for t in range(2):
+        warm_bank = psum.tile([P, N], F32, name="warm_bank", tag="value_1_0")
+        for i in range(2):
             nc.tensor.matmul_mx(
-                out=warm_bank[:],
-                lhsT=codes1[:, t * P : (t + 1) * P].bitcast(FP8X4),
-                lhsT_scale=plane1[:, t * P : (t + 1) * P],
+                out=warm_bank[0:32, :],
+                lhsT=codes1[:, i * P : i * P + 32].bitcast(FP8X4),
+                lhsT_scale=plane1[:, i * P : i * P + 32],
                 rhs=codes1[:].bitcast(FP8X4),
                 rhs_scale=plane1[:],
                 start=True,
@@ -157,7 +157,7 @@ def tile_picked_phglu_silu_po_kernel(
             step = HALF if s == 0 else width
             for lo in range(0, width, step):
                 tag = "gate_%d_%d" % (t0, c0 + lo)
-                bank = product(tag, codes1, plane1, t0, groups, c0 + lo, step, QUARTER if s else HALF)
+                bank = product(tag, codes1, plane1, t0, groups, c0 + lo, step, HALF)
                 nc.scalar.activation(out=gate[:, :, lo : lo + step], in_=bank[:], func=SILU)
             gates.append(gate)
             if s == 0:

@@ -87,7 +87,7 @@ def tile_picked_phglu_silu_po_kernel(
             )
 
         warm_bank = psum.tile([P, N], F32, name="warm_bank", tag="value_1_0")
-        for i in range(2):
+        for i in range(3):
             nc.tensor.matmul_mx(
                 out=warm_bank[0:32, :],
                 lhsT=codes1[:, i * P : i * P + 32].bitcast(FP8X4),

@@ -222,7 +222,7 @@ def tile_picked_phglu_silu_po_kernel(
                 )
             nc.sync.dma_start(out=y_words[:, h * HALF : (h + 1) * HALF], in_=y_codes[:].bitcast(I32))
         for quad in range(4):
-            queue = nc.sync if quad % 2 == 0 else nc.scalar
+            queue = nc.sync if quad == 0 else nc.scalar
             queue.dma_start(
                 out=out_2[0, 4 * quad : 4 * quad + 4, :].bitcast(I32),
                 in_=y_plane[32 * quad : 32 * quad + 4, :].bitcast(I32),

@@ -39,7 +39,7 @@ def tile_picked_phglu_silu_po_kernel(
         offsets = keep.tile([P, S // 16], U16, name="offsets")
         nc.sync.dma_start(offsets[:], offs)
         scale_table = reuse.tile([P, T], U8, name="scale_table", offset=HALF_W_BYTES, align_bytes=64)
-        nc.vector.memset(scale_table[:].bitcast(I32), 0)
+        nc.gpsimd.memset(scale_table[:].bitcast(I32), 0)
         nc.sync.dma_start(out=scale_table[0:P:8, :].bitcast(I32), in_=x_scales[0].bitcast(I32))
         nc.sync.dma_start(out=raw1[:, 2:4, :], in_=w1_rows[:, 2:4, :])
         word_table = keep.tile([P, T], U32, name="word_table", align_bytes=64)
@@ -62,7 +62,7 @@ def tile_picked_phglu_silu_po_kernel(
         picked_scales = keep.tile([P, S], U8, name="picked_scales", align_bytes=64)
         nc.vector.tensor_copy(out=picked_scales[:], in_=scale_table[:].indirect(offsets[:]))
         x_plane = keep.tile([P, S], U8, name="x_plane", align_bytes=64)
-        nc.gpsimd.memset(x_plane[:].bitcast(I32), 0)
+        nc.vector.memset(x_plane[:].bitcast(I32), 0)
         for quad in range(4):
             nc.sync.dma_start(
                 out=x_plane[32 * quad : 32 * quad + 4, :].bitcast(I32),

@@ -144,24 +144,29 @@ def tile_picked_phglu_silu_po_kernel(
         round_w2(nc.vector.tensor_copy, 0, 0)
         round_w2(nc.scalar.copy, 0, 1)
         quantize_w2(0)
-        round_w2(nc.vector.tensor_copy, 1, 0)
-        round_w2(nc.vector.tensor_copy, 1, 1, slice(0, HALF_GROUP // 2))
+        round_w2(nc.vector.tensor_copy, 1, 0, slice(0, 44))
+        round_w2(nc.vector.tensor_copy, 1, 1, slice(0, 44))
 
         sections = ((0, 1, 0, S), (1, 1, 0, S), (2, 2, 0, HALF), (2, 2, HALF, HALF))
 
-        first_gate = reuse.tile([P, S], F32, name="first_gate", offset=0, align_bytes=64)
-        later_gates = reuse.tile([P, 3, S], F32, name="later_gates", offset=HALF_W_BYTES + T, align_bytes=64)
+        first_gate = reuse.tile([P, HALF], F32, name="first_gate", offset=0, align_bytes=64)
+        later_gates = reuse.tile([P, 7 * HALF], F32, name="later_gates", offset=HALF_W_BYTES + T, align_bytes=64)
         gates = []
         for s, (t0, groups, c0, width) in enumerate(sections):
-            gate = (later_gates[:, s - 1, :] if s else first_gate[:]).rearrange("p (t c) -> p t c", t=groups)
-            step = HALF if s == 0 else width
-            for lo in range(0, width, step):
-                tag = "gate_%d_%d" % (t0, c0 + lo)
-                bank = product(tag, codes1, plane1, t0, groups, c0 + lo, step, HALF)
-                nc.scalar.activation(out=gate[:, :, lo : lo + step], in_=bank[:], func=SILU)
-            gates.append(gate)
             if s == 0:
-                round_w2(nc.scalar.copy, 1, 1, slice(HALF_GROUP // 2, HALF_GROUP))
+                halves = (first_gate[:], later_gates[:, 0:HALF])
+                for h in range(2):
+                    bank = product("gate_0_%d" % (h * HALF), codes1, plane1, 0, 1, h * HALF, HALF, HALF)
+                    nc.scalar.activation(out=halves[h], in_=bank[:, 0, :], func=SILU)
+                    if h == 0:
+                        round_w2(nc.scalar.copy, 1, 0, slice(44, HALF_GROUP))
+                        round_w2(nc.scalar.copy, 1, 1, slice(44, HALF_GROUP))
+                gates.append(halves)
+            else:
+                gate = later_gates[:, HALF + (s - 1) * S : HALF + s * S].rearrange("p (t c) -> p t c", t=groups)
+                bank = product("gate_%d_%d" % (t0, c0), codes1, plane1, t0, groups, c0, width, HALF)
+                nc.scalar.activation(out=gate, in_=bank[:], func=SILU)
+                gates.append(gate)
 
         quantize_w2(1)
 
@@ -178,7 +183,7 @@ def tile_picked_phglu_silu_po_kernel(
             if s == 0:
                 for lo in (0, HALF):
                     bank = product("value_0_%d" % lo, codes2, plane2, t0, groups, lo, HALF, HALF)
-                    gate_product(bank[:], s, lo, lo + HALF)
+                    nc.vector.tensor_tensor(out=y[:, 0, lo : lo + HALF], in0=bank[:, 0, :], in1=gates[0][lo // HALF], op=MULT)
             else:
                 tag = ("value_1_0", "gate_0_0", "gate_0_256")[s - 1]
                 bank = product(tag, codes2, plane2, t0, groups, c0, width, width)

@@ -215,8 +215,8 @@ def tile_picked_phglu_silu_po_kernel(
                 else:
                     copy = nc.vector.tensor_copy if q == 3 else nc.scalar.copy
                     copy(
-                        out=part.rearrange("p (c i) t -> p c t i", i=4),
-                        in_=y[:, :, places].rearrange("p t (c i) -> p c t i", i=4),
+                        out=part.rearrange("p (c i) t -> p c t i", i=2),
+                        in_=y[:, :, places].rearrange("p t (c i) -> p c t i", i=2),
                     )
             step = QUARTER if h else HALF
             for lo in range(0, HALF, step):

from contextlib import ExitStack

import concourse.mybir as mybir

K, T, S, N = 512, 2048, 512, 512
FLOPS = 2 * 2 * K * N * S

F32 = mybir.dt.float32
BF16 = mybir.dt.bfloat16
I32 = mybir.dt.int32
U32 = mybir.dt.uint32
U16 = mybir.dt.uint16
U8 = mybir.dt.uint8
FP8X4 = mybir.dt.float8_e4m3fn_x4
SILU = mybir.ActivationFunctionType.Silu
MULT = mybir.AluOpType.mult
ADD = mybir.AluOpType.add

P = 128
PACK = 4
QUARTER = S // 4
HALF = S // 2
HALF_W_BYTES = PACK * (N // 2) * 4
HALF_GROUP = P // 2


def tile_picked_phglu_silu_po_kernel(
    tc, x_words, x_scales, w1, w2, offs, out_0, out_1, out_2
):
    nc = tc.nc
    with ExitStack() as ctx:
        keep = ctx.enter_context(tc.tile_pool(name="keep", bufs=1))
        reuse = ctx.enter_context(tc.tile_pool(name="reuse", bufs=1))
        psum = ctx.enter_context(tc.psum_pool(name="psum", bufs=1))

        raw1 = keep.tile([P, PACK, N], F32, name="raw1", align_bytes=64)
        w1_rows = w1.rearrange("(p j) c -> p j c", j=PACK)
        nc.sync.dma_start(out=raw1[:, 0:2, :], in_=w1_rows[:, 0:2, :])
        offsets = keep.tile([P, S // 16], U16, name="offsets")
        nc.sync.dma_start(offsets[:], offs)
        scale_table = reuse.tile([P, T], U8, name="scale_table", offset=HALF_W_BYTES, align_bytes=64)
        nc.gpsimd.memset(scale_table[:].bitcast(I32), 0)
        nc.sync.dma_start(out=scale_table[0:P:8, :].bitcast(I32), in_=x_scales[0].bitcast(I32))
        nc.sync.dma_start(out=raw1[:, 2:4, :], in_=w1_rows[:, 2:4, :])
        word_table = keep.tile([P, T], U32, name="word_table", align_bytes=64)
        nc.sync.dma_start(
            out=word_table[:].bitcast(I32), in_=x_words[0].rearrange("p c r -> p (c r)").bitcast(I32)
        )

        warm = keep.tile([P, 2], F32, name="warm")
        nc.vector.memset(warm[:, 0:1], 0.0)
        nc.scalar.activation(out=warm[:, 1:2], in_=warm[:, 0:1], func=SILU)

        w2_rows = w2.rearrange("(p j) c -> p j c", j=PACK)
        raw2 = {}

        def load_w2(c):
            raw2[c] = reuse.tile([P, PACK, N // 2], F32, name="raw2_%d" % c, offset=HALF_W_BYTES * c, align_bytes=64)
            nc.sync.dma_start(out=raw2[c][:], in_=w2_rows[:, :, c * N // 2 : (c + 1) * N // 2])

        load_w2(0)
        picked_scales = keep.tile([P, S], U8, name="picked_scales", align_bytes=64)
        nc.vector.tensor_copy(out=picked_scales[:], in_=scale_table[:].indirect(offsets[:]))
        x_plane = keep.tile([P, S], U8, name="x_plane", align_bytes=64)
        nc.vector.memset(x_plane[:].bitcast(I32), 0)
        for quad in range(4):
            nc.sync.dma_start(
                out=x_plane[32 * quad : 32 * quad + 4, :].bitcast(I32),
                in_=picked_scales[32 * quad : 32 * quad + 32 : 8, :].bitcast(I32),
            )
        load_w2(1)

        dealt1 = [keep.tile([P, 2, P, PACK], BF16, name="dealt1", tag="dealt1_%d" % u, align_bytes=64) for u in range(2)]
        for u, copy in enumerate((nc.vector.tensor_copy, nc.scalar.copy)):
            copy(
                out=dealt1[u][:].rearrange("p t m j -> p m j t"),
                in_=raw1[:].rearrange("p j (m t) -> p m j t", t=PACK)[:, :, :, 2 * u : 2 * u + 2],
            )
        codes1 = keep.tile([P, N], U32, name="codes1", align_bytes=64)
        plane1 = keep.tile([P, N], U8, name="plane1", align_bytes=64)
        for u in range(2):
            cols = slice(2 * u * P, 2 * (u + 1) * P)
            nc.vector.quantize_mx(
                out=codes1[:, cols].bitcast(FP8X4),
                scales=plane1[:, cols],
                in_=dealt1[u][:].rearrange("p t m j -> p (t m j)"),
            )

        warm_bank = psum.tile([P, N], F32, name="warm_bank", tag="value_1_0")
        for i in range(3):
            nc.tensor.matmul_mx(
                out=warm_bank[0:32, :],
                lhsT=codes1[:, i * P : i * P + 32].bitcast(FP8X4),
                lhsT_scale=plane1[:, i * P : i * P + 32],
                rhs=codes1[:].bitcast(FP8X4),
                rhs_scale=plane1[:],
                start=True,
                stop=True,
            )

        picked = keep.tile([P, S], U32, name="picked", tag="dealt1_1", align_bytes=64)
        for h in range(2):
            nc.vector.tensor_copy(
                out=picked[:, h * HALF : (h + 1) * HALF],
                in_=word_table[:].indirect(offsets[:, h * HALF // 16 : (h + 1) * HALF // 16]),
            )

        def product(tag, codes, plane, t0, groups, c0, width, step):
            bank = psum.tile([P, groups, width], F32, name="bank", tag=tag)
            for t in range(t0, t0 + groups):
                for lo in range(0, width, step):
                    nc.tensor.matmul_mx(
                        out=bank[:, t - t0, lo : lo + step],
                        lhsT=codes[:, t * P : (t + 1) * P].bitcast(FP8X4),
                        lhsT_scale=plane[:, t * P : (t + 1) * P],
                        rhs=picked[:, c0 + lo : c0 + lo + step].bitcast(FP8X4),
                        rhs_scale=x_plane[:, c0 + lo : c0 + lo + step],
                        start=True,
                        stop=True,
                    )
            return bank

        codes2 = keep.tile([P, N], U32, name="codes2", align_bytes=64)
        plane2 = keep.tile([P, N], U8, name="plane2", align_bytes=64)
        dealt2 = {}

        def round_w2(copy, c, u, part=slice(0, HALF_GROUP)):
            if (c, u) not in dealt2:
                dealt2[c, u] = keep.tile([P, 2, HALF_GROUP, PACK], BF16, name="dealt2_%d_%d" % (c, u), align_bytes=64)
            copy(
                out=dealt2[c, u][:, :, part].rearrange("p t m j -> p m j t"),
                in_=raw2[c][:].rearrange("p j (m t) -> p m j t", t=PACK)[:, part, :, 2 * u : 2 * u + 2],
            )

        def quantize_w2(c):
            for t in range(PACK):
                cols = slice(t * P + c * HALF_GROUP, t * P + (c + 1) * HALF_GROUP)
                nc.vector.quantize_mx(
                    out=codes2[:, cols].bitcast(FP8X4),
                    scales=plane2[:, cols],
                    in_=dealt2[c, t // 2][:, t % 2].rearrange("p m j -> p (m j)"),
                )

        round_w2(nc.vector.tensor_copy, 0, 0)
        round_w2(nc.scalar.copy, 0, 1)
        quantize_w2(0)
        round_w2(nc.vector.tensor_copy, 1, 0, slice(0, 44))
        round_w2(nc.vector.tensor_copy, 1, 1, slice(0, 44))

        sections = ((0, 1, 0, S), (1, 1, 0, S), (2, 2, 0, HALF), (2, 2, HALF, HALF))

        first_gate = reuse.tile([P, HALF], F32, name="first_gate", offset=0, align_bytes=64)
        later_gates = reuse.tile([P, 7 * HALF], F32, name="later_gates", offset=HALF_W_BYTES + T, align_bytes=64)
        gates = []
        for s, (t0, groups, c0, width) in enumerate(sections):
            if s == 0:
                halves = (first_gate[:], later_gates[:, 0:HALF])
                for h in range(2):
                    bank = product("gate_0_%d" % (h * HALF), codes1, plane1, 0, 1, h * HALF, HALF, HALF)
                    nc.scalar.activation(out=halves[h], in_=bank[:, 0, :], func=SILU)
                    if h == 0:
                        round_w2(nc.scalar.copy, 1, 0, slice(44, HALF_GROUP))
                        round_w2(nc.scalar.copy, 1, 1, slice(44, HALF_GROUP))
                gates.append(halves)
            else:
                gate = later_gates[:, HALF + (s - 1) * S : HALF + s * S].rearrange("p (t c) -> p t c", t=groups)
                bank = product("gate_%d_%d" % (t0, c0), codes1, plane1, t0, groups, c0, width, HALF)
                nc.scalar.activation(out=gate, in_=bank[:], func=SILU)
                gates.append(gate)

        quantize_w2(1)

        y_rows = out_0.rearrange("(p t) j -> p t j", t=PACK)
        y = keep.tile([P, PACK, S], F32, name="y", align_bytes=64)

        def gate_product(bank, s, lo, hi):
            t0, groups, c0, width = sections[s]
            nc.vector.tensor_tensor(
                out=y[:, t0 : t0 + groups, c0 + lo : c0 + hi], in0=bank, in1=gates[s][:, :, lo:hi], op=MULT
            )

        for s, (t0, groups, c0, width) in enumerate(sections):
            if s == 0:
                for lo in (0, HALF):
                    bank = product("value_0_%d" % lo, codes2, plane2, t0, groups, lo, HALF, HALF)
                    nc.vector.tensor_tensor(out=y[:, 0, lo : lo + HALF], in0=bank[:, 0, :], in1=gates[0][lo // HALF], op=MULT)
            else:
                tag = ("value_1_0", "gate_0_0", "gate_0_256")[s - 1]
                bank = product(tag, codes2, plane2, t0, groups, c0, width, width)
                step = width // groups
                for lo in range(0, width, step):
                    gate_product(bank[:, :, lo : lo + step], s, lo, lo + step)
            nc.sync.dma_start(
                out=y_rows[:, t0 : t0 + groups, c0 : c0 + width], in_=y[:, t0 : t0 + groups, c0 : c0 + width]
            )

        y_words = out_1[0].rearrange("p c r -> p (c r)").bitcast(I32)
        y_plane = keep.tile([P, S], U8, name="y_plane", align_bytes=64)
        for h in range(2):
            y_codes = keep.tile([P, HALF], U32, name="y_codes%d" % h, align_bytes=64)
            rounded = keep.tile([P, HALF, PACK], BF16, name="rounded%d" % h, align_bytes=64)
            for u in range(2):
                q = 2 * h + u
                places = slice(q * QUARTER, (q + 1) * QUARTER)
                part = rounded[:, u * QUARTER : (u + 1) * QUARTER, :]
                if q == 0:
                    nc.gpsimd.tensor_scalar(
                        out=part,
                        in0=y[:, :, places].rearrange("p t c -> p c t"),
                        scalar1=1.0,
                        scalar2=-0.0,
                        op0=MULT,
                        op1=ADD,
                    )
                else:
                    copy = nc.vector.tensor_copy if q == 3 else nc.scalar.copy
                    copy(
                        out=part.rearrange("p (c i) t -> p c t i", i=2),
                        in_=y[:, :, places].rearrange("p t (c i) -> p c t i", i=2),
                    )
            step = QUARTER if h else HALF
            for lo in range(0, HALF, step):
                nc.vector.quantize_mx(
                    out=y_codes[:, lo : lo + step].bitcast(FP8X4),
                    scales=y_plane[:, h * HALF + lo : h * HALF + lo + step],
                    in_=rounded[:, lo : lo + step, :].rearrange("p c t -> p (c t)"),
                )
            nc.sync.dma_start(out=y_words[:, h * HALF : (h + 1) * HALF], in_=y_codes[:].bitcast(I32))
        for quad in range(4):
            queue = nc.sync if quad == 0 else nc.scalar
            queue.dma_start(
                out=out_2[0, 4 * quad : 4 * quad + 4, :].bitcast(I32),
                in_=y_plane[32 * quad : 32 * quad + 4, :].bitcast(I32),
            )
